import numpy as np
import ml_dtypes


def mxq(x, axis, fmt="e4m3"):
    dtype, down = {"e4m3": (ml_dtypes.float8_e4m3fn, 7), "e5m2": (ml_dtypes.float8_e5m2, 14)}[fmt]
    v = np.moveaxis(np.asarray(x, np.float32).astype(ml_dtypes.bfloat16).astype(np.float64), axis, -1)
    blocks = v.reshape(v.shape[:-1] + (-1, 32))
    amax = np.abs(blocks).max(-1, keepdims=True)
    byte = np.maximum(np.where(amax > 0, np.frexp(amax)[1] - 1 + 127, 0) - down, 1)
    scale = np.exp2(byte - 127.0)
    codes = (blocks / scale).astype(np.float32).astype(dtype).astype(np.float64)
    return np.moveaxis((codes * scale).reshape(v.shape), -1, axis)


WIDE = False


def mx_kscale(k):
    if not WIDE:
        return np.ones(k)
    levels = np.array([10, -10, 5, -5, 0])
    if k % 512:
        return np.exp2(np.random.permutation(np.resize(levels, k // 32))).repeat(32)
    a = np.empty((k // 512, 16))
    for p in range(k // 512):
        a[p, :8] = np.random.permutation(np.resize(levels, 8))
        for g in range(8):
            far = levels[np.abs(levels - a[p, g]) >= 10]
            a[p, g + 8] = far[np.random.randint(len(far))]
    return np.exp2(a.ravel()).repeat(32)


BF16 = ml_dtypes.bfloat16


def bf(x):
    return np.asarray(x, np.float32).astype(BF16)


def f64(x):
    return np.asarray(x).astype(np.float64)


Q, B, N, D, E, K = 512, 128, 16, 512, 512, 6
N1 = N + 1


def draw0():
    s = mx_kscale(D)
    t = mx_kscale(E)
    q = 1.4 * np.random.standard_normal((Q, E)) / np.sqrt(E) / t
    topic = 0.8 * np.random.standard_normal((B, 1, D))
    x = (topic + 0.6 * np.random.standard_normal((B, N1, D))) * s
    w = np.random.standard_normal((2, D, E)) / np.sqrt(2 * D) / s[None, :, None]
    bias = 0.3 * np.random.standard_normal(E)
    gain = np.random.standard_normal(E) * t
    mu = np.random.uniform(-1.5, 1.5, K)
    sigma = np.random.uniform(0.5, 0.9, K)
    return {"q": bf(q), "x": bf(x), "w": bf(w), "bias": bf(bias), "gain": bf(gain), "mu": bf(mu), "sigma": bf(sigma)}


def bigram_features(x, w, bias, gain):
    xq = mxq(f64(x), 2, "e4m3")
    wq = mxq(f64(w), 1, "e4m3")
    xa = xq[:, 0:N, :].reshape(B * N, D)
    xb = xq[:, 1:N + 1, :].reshape(B * N, D)
    h = (xa @ wq[0]) + (xb @ wq[1]) + f64(bias)
    return np.maximum(h, 0.0) * f64(gain)


def log_mean_exp_over_n(z):
    n = z.shape[2]
    m = np.max(z, axis=2, keepdims=True)
    total = np.sum(np.exp(z - m), axis=2)
    lse = np.log(total) + np.squeeze(m, axis=2)
    return lse - np.log(n)


def core(q, x, w, bias, gain, mu, sigma):
    d = bigram_features(x, w, bias, gain)
    sc = (mxq(f64(q), 1, "e4m3") @ mxq(d, 1, "e4m3").T).reshape(Q, B, N)
    diff = sc[:, :, :, None] - f64(mu)
    sg = f64(sigma)
    z = -(diff * diff) / (2.0 * (sg * sg))
    return log_mean_exp_over_n(z)


def e4m3fn_bytes(y):
    return np.clip(np.asarray(y, np.float64), -448.0, 448.0).astype(np.float32).astype(ml_dtypes.float8_e4m3fn).view(np.uint8)


def e4m3fn_values(b):
    return np.asarray(b, np.uint8).view(ml_dtypes.float8_e4m3fn).astype(np.float64)


def setup_inputs():
    d = draw0()
    x0 = np.asarray(d['x']).astype(np.float64)
    s = (np.max(np.abs(x0), axis=(0, 1), keepdims=True) / 448.0).astype(np.float32)
    out = {}
    for k, v in d.items():
        if k == 'x':
            out['x_bytes'] = e4m3fn_bytes(x0 / s.astype(np.float64))
            out['x_scale'] = s
        else:
            out[k] = v
    return out


def reference(q, x_bytes, x_scale, w, bias, gain, mu, sigma):
    return core(q, e4m3fn_values(x_bytes) * x_scale.astype(np.float64), w, bias, gain, mu, sigma)

@@ -1,0 +1,438 @@
+import math
+from contextlib import ExitStack
+
+import concourse.mybir as mybir
+from concourse.masks import make_identity
+
+Q, B, N, D, E, K = 512, 128, 16, 512, 512, 6
+FLOPS = 2 * 2 * (B * N) * D * E + 2 * Q * (B * N) * E
+
+F32 = mybir.dt.float32
+BF16 = mybir.dt.bfloat16
+U32 = mybir.dt.uint32
+U8 = mybir.dt.uint8
+FP8 = mybir.dt.float8_e4m3fn
+FP8X4 = mybir.dt.float8_e4m3fn_x4
+ACT = mybir.ActivationFunctionType
+ALU = mybir.AluOpType
+
+P = 128
+T = 4
+NQ = Q // P
+GROUPS = (2, 2, 4, 4, 4)
+UNITS = ((0, 2), (2, 1), (3, 2), (5, 2), (7, 2), (9, 2), (11, 2), (13, 2), (15, 2))
+UNITS_OF_GROUP = ((0, 1), (2,), (3, 4), (5, 6), (7, 8))
+RELU_ON_VECTOR = [[],[],[1],[1,3],[1,2,3]]
+COPY_ON_VECTOR = [0,0,0,0,0,0,0,0,0]
+COLLECT_ON_SCALAR = []
+
+
+def tile_bigramconvkernelpoolingmatch_kernel(tc, q, x_bytes, x_scale, w, bias, gain, mu, sigma, out):
+    nc = tc.nc
+    with ExitStack() as ctx:
+        keep = ctx.enter_context(tc.tile_pool(name="keep", bufs=1))
+        work = ctx.enter_context(tc.tile_pool(name="work", bufs=2))
+        u_pool = ctx.enter_context(tc.tile_pool(name="u", bufs=12))
+        psum = ctx.enter_context(tc.psum_pool(name="psum", bufs=3))
+        ctx.enter_context(tc.manual_schedule())
+
+        x_raw = keep.tile([P, (N + 1) * D], U8)
+        x_rows = x_bytes.rearrange("b n d -> b (n d)")
+        scale_bc = keep.tile([P, D], F32)
+        w_raw = [keep.tile([P, T, E], BF16, name="w_raw%d" % tap) for tap in range(2)]
+        gain_pt = keep.tile([P, T], BF16)
+        bias_pt = keep.tile([P, T], BF16)
+        q_rows = keep.tile([P, NQ, E], BF16)
+        gain_bc = keep.tile([P, E], BF16)
+        mu_bc = keep.tile([P, K], BF16)
+        sigma_bc = keep.tile([P, K], BF16)
+
+        def load_x(a, b):
+            nc.sync.dma_start(out=x_raw[:, a * D : b * D], in_=x_rows[:, a * D : b * D])
+
+        def load_w(tap):
+            nc.sync.dma_start(out=w_raw[tap][:], in_=w[tap].rearrange("(p j) e -> p j e", j=T))
+
+        nc.scalar.dma_start(out=scale_bc[:], in_=x_scale.rearrange("a b d -> (a b d)").partition_broadcast(P))
+        load_x(0, 3)
+        load_w(0)
+        load_w(1)
+        nc.scalar.dma_start(out=gain_pt[:], in_=gain.rearrange("(p t) -> p t", t=T))
+        nc.scalar.dma_start(out=bias_pt[:], in_=bias.rearrange("(p t) -> p t", t=T))
+        load_x(3, 5)
+        nc.sync.dma_start(out=q_rows[:], in_=q.rearrange("(c r) e -> r c e", r=P))
+        load_x(5, 9)
+        nc.scalar.dma_start(out=gain_bc[:], in_=gain.partition_broadcast(P))
+        nc.scalar.dma_start(out=mu_bc[:], in_=mu.partition_broadcast(P))
+        nc.scalar.dma_start(out=sigma_bc[:], in_=sigma.partition_broadcast(P))
+        load_x(9, 17)
+
+        ident = keep.tile([P, P], F32)
+        make_identity(nc, ident[:])
+
+        warm = keep.tile([P, 1], F32)
+        nc.vector.memset(warm[:], 1.0)
+        nc.scalar.activation(out=warm[:], in_=warm[:], func=ACT.Exp)
+
+        def turn(src, count, dst, on_vector):
+            xt = psum.tile([P, 2, 2, P], F32, name="xt", tag="p", bufs=3)
+            words = src.bitcast(F32)
+            for r in range(count):
+                base = 256 * r
+                for u in range(2):
+                    nc.tensor.transpose(xt[:, r, u, :], words[:, base + u : base + 256 : 2], ident[:])
+            o = dst.bitcast(F32).rearrange("p (b r u) -> p b r u", b=count, u=2)
+            i = xt[:, 0:count].rearrange("p b u r -> p b r u")
+            if on_vector:
+                nc.vector.tensor_copy(out=o, in_=i)
+            else:
+                nc.scalar.copy(out=o, in_=i)
+
+        x_codes = keep.tile([P, (N + 1) * B], U32, align_bytes=64)
+        x_scales = keep.tile([P, (N + 1) * B], U8, align_bytes=64)
+        xs_of, xg_of = {}, {}
+
+        def x_widen(unit):
+            first, count = UNITS[unit]
+            xs = work.tile([P, 2 * D], BF16, name="xs", bufs=3)
+            for r in range(count):
+                n = first + r
+                nc.vector.tensor_tensor(out=xs[:, r * D : (r + 1) * D], in0=x_raw[:, n * D : (n + 1) * D].bitcast(FP8), in1=scale_bc[:], op=ALU.mult)
+            xs_of[unit] = xs
+
+        def x_turn(unit):
+            count = UNITS[unit][1]
+            xg = work.tile([P, 2 * B * T], BF16, name="xg", bufs=3, align_bytes=64)
+            turn(xs_of[unit][:], count, xg[:, 0 : count * B * T], COPY_ON_VECTOR[unit])
+            xg_of[unit] = xg
+
+        def x_quantize(unit):
+            first, count = UNITS[unit]
+            cols = slice(first * B, (first + count) * B)
+            nc.vector.quantize_mx(out=x_codes[:, cols].bitcast(FP8X4), scales=x_scales[:, cols], in_=xg_of[unit][:, 0 : count * B * T])
+
+        w_codes, w_scales = [], []
+        grouped_w = {}
+
+        def w_group(tap):
+            grouped = work.tile([P, T * P, T], BF16, name="w_grouped", align_bytes=64)
+            src = w_raw[tap][:].rearrange("p j (m t) -> p t m j", t=T)
+            dst = grouped[:].rearrange("p (t m) j -> p t m j", t=T)
+            cut = T if tap == 0 else 2
+            nc.vector.tensor_copy(out=dst[:, 0:cut], in_=src[:, 0:cut])
+            if cut < T:
+                nc.scalar.copy(out=dst[:, cut:T], in_=src[:, cut:T])
+            grouped_w[tap] = grouped
+
+        def w_quantize(tap):
+            codes = keep.tile([P, E], U32, name="w_codes%d" % tap, align_bytes=64)
+            scales = keep.tile([P, E], U8, name="w_scales%d" % tap, align_bytes=64)
+            nc.vector.quantize_mx(out=codes[:].bitcast(FP8X4), scales=scales[:], in_=grouped_w[tap][:].rearrange("p c j -> p (c j)"))
+            w_codes.append(codes)
+            w_scales.append(scales)
+
+        q_codes = keep.tile([P, Q], U32, align_bytes=64)
+        q_scales = keep.tile([P, Q], U8, align_bytes=64)
+        q_parts = {}
+
+        def q_sign():
+            qs = work.tile([P, NQ, E], BF16, name="qs", tag="relu")
+            nc.vector.tensor_tensor(out=qs[:], in0=q_rows[:], in1=sign_bc[:].unsqueeze(1).to_broadcast([P, NQ, E]), op=ALU.mult)
+            qg = work.tile([P, Q * T], BF16, name="qg", tag="d_grouped", align_bytes=64)
+            q_parts[0] = (qs, qg)
+
+        def q_turn():
+            qs, qg = q_parts[0]
+            for h in range(2):
+                turn(qs[:, 2 * h : 2 * h + 2, :].rearrange("p c e -> p (c e)"), 2, qg[:, h * 1024 : (h + 1) * 1024], False)
+
+        def q_quantize():
+            nc.vector.quantize_mx(out=q_codes[:].bitcast(FP8X4), scales=q_scales[:], in_=q_parts[0][1][:])
+
+        d_codes = keep.tile([P, N * B], U32, align_bytes=64)
+        d_scales = keep.tile([P, N * B], U8, align_bytes=64)
+        relu_of, grouped_of, h_of = {}, {}, {}
+        first_of = [sum(GROUPS[:g]) for g in range(len(GROUPS))]
+
+        def convolve(g):
+            width_n = GROUPS[g] * B
+            lo = first_of[g] * B
+            relu = work.tile([P, T, 4 * B], BF16, name="relu", tag="relu")
+            relu_of[g] = relu
+            for t in range(T):
+                h = psum.tile([P, 4 * B], F32, name="h", tag=("p", "r")[t % 2], bufs=(3, 2)[t % 2])
+                for tap in range(2):
+                    cols = slice(lo + tap * B, lo + tap * B + width_n)
+                    nc.tensor.matmul_mx(
+                        out=h[:, 0:width_n],
+                        lhsT=w_codes[tap][:, t * P : (t + 1) * P].bitcast(FP8X4),
+                        lhsT_scale=w_scales[tap][:, t * P : (t + 1) * P],
+                        rhs=x_codes[:, cols].bitcast(FP8X4),
+                        rhs_scale=x_scales[:, cols],
+                        start=(tap == 0),
+                        stop=(tap == 1),
+                    )
+                h_of[g, t] = h
+                if t not in RELU_ON_VECTOR[g]:
+                    nc.scalar.activation(out=relu[:, t, 0:width_n], in_=h[:, 0:width_n], func=ACT.Identity, bias=gain_bias[:, t : t + 1], scale=abs_gain[:, t : t + 1])
+
+        def affine_on_vector(g):
+            width_n = GROUPS[g] * B
+            for t in RELU_ON_VECTOR[g]:
+                nc.vector.tensor_scalar(out=relu_of[g][:, t, 0:width_n], in0=h_of[g, t][:, 0:width_n], scalar1=abs_gain[:, t : t + 1], scalar2=gain_bias[:, t : t + 1], op0=ALU.mult, op1=ALU.add)
+
+        def d_group(g):
+            width_n = GROUPS[g] * B
+            grouped = work.tile([P, 4 * B, T], BF16, name="d_grouped", tag="d_grouped", align_bytes=64)
+            nc.vector.tensor_scalar(out=grouped[:, 0:width_n, :], in0=relu_of[g][:, :, 0:width_n].rearrange("p t n -> p n t"), scalar1=0.0, scalar2=None, op0=ALU.max)
+            grouped_of[g] = grouped
+
+        def d_quantize(g):
+            width_n = GROUPS[g] * B
+            lo = first_of[g] * B
+            nc.vector.quantize_mx(out=d_codes[:, lo : lo + width_n].bitcast(FP8X4), scales=d_scales[:, lo : lo + width_n], in_=grouped_of[g][:, 0:width_n, :].rearrange("p n t -> p (n t)"))
+
+        steps = 2 * K
+        us, lows, negs, rs, res, t1s, flips = {}, {}, {}, {}, {}, {}, {}
+
+        def scores(block, side, first, count):
+            bank = psum.tile([P, 4, P], F32, name="s", tag="s", bufs=3)
+            q_cols = slice(block * P, (block + 1) * P)
+            if side == 0:
+                cols = slice(first * B, (first + count) * B)
+                nc.tensor.matmul_mx(
+                    out=bank[:, 0:count, :],
+                    lhsT=q_codes[:, q_cols].bitcast(FP8X4),
+                    lhsT_scale=q_scales[:, q_cols],
+                    rhs=d_codes[:, cols].bitcast(FP8X4),
+                    rhs_scale=d_scales[:, cols],
+                    start=True,
+                    stop=True,
+                )
+            else:
+                for i in range(count):
+                    cols = slice((first + i) * B, (first + i + 1) * B)
+                    nc.tensor.matmul_mx(
+                        out=bank[:, i, :],
+                        lhsT=d_codes[:, cols].bitcast(FP8X4),
+                        lhsT_scale=d_scales[:, cols],
+                        rhs=q_codes[:, q_cols].bitcast(FP8X4),
+                        rhs_scale=q_scales[:, q_cols],
+                        start=True,
+                        stop=True,
+                    )
+            return bank
+
+        def new_u(s, side):
+            us[s, side] = u_pool.tile([P, N, P], F32, name="u", tag="u", bufs=12)
+
+        def square(s, side, bank, first, count):
+            k = s % K
+            nc.scalar.activation(out=us[s, side][:, first : first + count, :], in_=bank[:, 0:count, :], func=ACT.Square, bias=centre[:, k : k + 1], scale=width[:, k : k + 1])
+
+        def first_half(s):
+            for side in range(2):
+                t1 = work.tile([P, 2, 4, P], F32, name="t1", bufs=3)
+                nc.vector.tensor_tensor(out=t1[:, 0], in0=us[s, side][:, 0:4, :], in1=us[s, side][:, 4:8, :], op=ALU.min)
+                t1s[s, side] = t1
+
+        def level_one(s):
+            for side in range(2):
+                u = us[s, side]
+                if (s, side) in t1s:
+                    nc.vector.tensor_tensor(out=t1s[s, side][:, 1], in0=u[:, 8:12, :], in1=u[:, 12:16, :], op=ALU.min)
+                else:
+                    t1 = work.tile([P, 2, 4, P], F32, name="t1", bufs=3)
+                    v = u[:].rearrange("p (h a n) c -> p h a n c", h=2, a=2)
+                    nc.vector.tensor_tensor(out=t1[:], in0=v[:, :, 0], in1=v[:, :, 1], op=ALU.min)
+                    t1s[s, side] = t1
+
+        def levels_two_to_four(s):
+            t2s, t3s = [], []
+            for side in range(2):
+                t2 = work.tile([P, 4, P], F32, name="t2")
+                nc.vector.tensor_tensor(out=t2[:], in0=t1s[s, side][:, 0], in1=t1s[s, side][:, 1], op=ALU.min)
+                t2s.append(t2)
+            for side in range(2):
+                t3 = work.tile([P, 2, P], F32, name="t3")
+                nc.vector.tensor_tensor(out=t3[:], in0=t2s[side][:, 0:2, :], in1=t2s[side][:, 2:4, :], op=ALU.min)
+                t3s.append(t3)
+            if s % K == 0:
+                r = keep.tile([P, 4, K, P], F32, name="res%d" % (s // K))
+                res[s // K] = r
+            low0 = res[s // K][:, 3, s % K, :]
+            low1 = work.tile([P, P], F32, name="low", bufs=3)
+            lows[s] = low1
+            neg = work.tile([P, P], F32, name="neg", bufs=3)
+            negs[s] = neg
+            for side, low in ((0, low0), (1, low1[:])):
+                nc.vector.tensor_tensor(out=low, in0=t3s[side][:, 0, :], in1=t3s[side][:, 1, :], op=ALU.min)
+            nc.vector.tensor_scalar(out=neg[:], in0=low0, scalar1=-1.0, scalar2=None, op0=ALU.mult)
+
+        def shift(s):
+            u = us[s, 1]
+            nc.vector.tensor_tensor(out=u[:], in0=u[:], in1=lows[s][:].unsqueeze(1).to_broadcast([P, N, P]), op=ALU.subtract)
+
+        def exp_shifted(s):
+            u = us[s, 1]
+            nc.scalar.activation(out=u[:], in_=u[:], func=ACT.Exp, scale=-1.0)
+
+        def flip_turn(s, j):
+            bank = psum.tile([P, 4, P], F32, name="f", tag="p", bufs=3)
+            for i in range(4):
+                nc.tensor.matmul(out=bank[:, i, :], lhsT=us[s, 0][:, 4 * j + i, :], rhs=ident[:], is_transpose=True, start=True, stop=False)
+                nc.tensor.matmul(out=bank[:, i, :], lhsT=negs[s][:], rhs=ident[:], is_transpose=True, start=False, stop=True)
+            flips[s, j] = bank
+
+        def flip_exp(s, j):
+            nc.scalar.activation(out=us[s, 0][:, 4 * j : 4 * j + 4, :], in_=flips[s, j][:], func=ACT.Exp, scale=-1.0)
+
+        def sums(s, side):
+            if side == 0:
+                r = psum.tile([P, 3, P], F32, name="r", tag="r", bufs=2)
+                rs[s] = r
+                nc.tensor.transpose(r[:, 2, :], lows[s][:], ident[:])
+            for n in range(N):
+                nc.tensor.matmul(out=rs[s][:, side, :], lhsT=us[s, side][:, n, :], rhs=ident[:], is_transpose=True, start=(n == 0), stop=(n == N - 1))
+
+        def collect(s):
+            o = res[s // K][:, 0:3, s % K, :]
+            if s in COLLECT_ON_SCALAR:
+                nc.scalar.copy(out=o, in_=rs[s][:])
+            else:
+                nc.vector.tensor_copy(out=o, in_=rs[s][:])
+
+        def logarithm(half, k0, k1):
+            r = res[half]
+            nc.scalar.activation(out=r[:, 0:2, k0:k1, :], in_=r[:, 0:2, k0:k1, :], func=ACT.Ln)
+
+        def finish(half):
+            r = res[half]
+            for side, low in ((0, 3), (1, 2)):
+                block = 2 * half + side
+                o = work.tile([P, B, K], F32, name="o")
+                nc.vector.scalar_tensor_tensor(
+                    out=o[:],
+                    in0=r[:, side].rearrange("p k b -> p b k"),
+                    scalar=-math.log(N),
+                    in1=r[:, low].rearrange("p k b -> p b k"),
+                    op0=ALU.add,
+                    op1=ALU.subtract,
+                )
+                nc.sync.dma_start(out=out[block * P : (block + 1) * P], in_=o[:])
+
+        abs_gain = keep.tile([P, T], F32)
+        gain_bias = keep.tile([P, T], F32)
+        sign_bc = keep.tile([P, E], BF16)
+        width = keep.tile([P, K], F32)
+        centre = keep.tile([P, K], F32)
+
+        x_widen(0)
+        x_widen(1)
+        x_turn(0)
+        x_turn(1)
+        w_group(0)
+        x_quantize(0)
+        x_quantize(1)
+        w_group(1)
+        w_quantize(0)
+        nc.vector.scalar_tensor_tensor(out=abs_gain[:], in0=gain_pt[:], scalar=-1.0, in1=gain_pt[:], op0=ALU.mult, op1=ALU.max)
+        w_quantize(1)
+        nc.vector.tensor_tensor(out=gain_bias[:], in0=abs_gain[:], in1=bias_pt[:], op=ALU.mult)
+        nc.vector.tensor_scalar(out=sign_bc[:], in0=gain_bc[:], scalar1=0.0, scalar2=2.0, op0=ALU.is_ge, op1=ALU.mult)
+        x_widen(2)
+        convolve(0)
+        x_turn(2)
+        nc.vector.tensor_scalar(out=sign_bc[:], in0=sign_bc[:], scalar1=-1.0, scalar2=None, op0=ALU.add)
+        nc.vector.reciprocal(out=width[:], in_=sigma_bc[:])
+        q_sign()
+        q_turn()
+        nc.vector.tensor_scalar(out=width[:], in0=width[:], scalar1=math.sqrt(0.5), scalar2=None, op0=ALU.mult)
+        x_quantize(2)
+        nc.vector.scalar_tensor_tensor(out=centre[:], in0=mu_bc[:], scalar=-1.0, in1=width[:], op0=ALU.mult, op1=ALU.mult)
+        q_late = [q_quantize]
+        for s in range(K):
+            for side in range(2):
+                new_u(s, side)
+
+        def units_of(g):
+            return UNITS_OF_GROUP[g] if g < len(GROUPS) else ()
+
+        for g in range(len(GROUPS)):
+            last = g + 1 == len(GROUPS)
+            if not last:
+                convolve(g + 1)
+            nxt = units_of(g + 2)
+            d_group(g)
+            for unit in nxt[0:1]:
+                x_widen(unit)
+                x_turn(unit)
+            d_quantize(g)
+            if g == 0:
+                q_quantize()
+            banks = [scores(side, side, first_of[g], GROUPS[g]) for side in range(2)]
+            if not last:
+                affine_on_vector(g + 1)
+            for unit in nxt[1:2]:
+                x_widen(unit)
+                x_turn(unit)
+            for unit in nxt:
+                x_quantize(unit)
+            for s in range(K):
+                for side in range(2):
+                    square(s, side, banks[side], first_of[g], GROUPS[g])
+        for s in range(1):
+            first_half(s)
+
+        def vector_work(s):
+            ahead = s + 2
+            if ahead < steps:
+                level_one(ahead)
+            if 0 <= ahead - 1 < steps:
+                shift(ahead - 1)
+            if ahead < steps:
+                levels_two_to_four(ahead)
+            if 1 <= s <= steps:
+                collect(s - 1)
+
+        for s in range(-2, 0):
+            vector_work(s)
+        for j in range(3):
+            flip_turn(0, j)
+        for s in range(steps + 1):
+            vector_work(s)
+            if s == 8:
+                logarithm(0, 0, K)
+                finish(0)
+            if s == steps:
+                break
+            fresh = []
+            if 1 <= s <= K:
+                base = K + (s - 1) // 2 * 2
+                side = (s - 1) % 2
+                block = 2 + side
+                fresh = [base, base + 1]
+                for f in fresh:
+                    new_u(f, side)
+            flip_turn(s, 3)
+            banks = [scores(block, side, 4 * j, 4) for j in range(2)] if fresh else []
+            for j in range(4):
+                flip_exp(s, j)
+            sums(s, 0)
+            for j in range(2 if fresh else 0):
+                for f in fresh:
+                    square(f, side, banks[j], 4 * j, 4)
+            if fresh:
+                banks += [scores(block, side, 4 * j, 4) for j in range(2, 4)]
+            if s + 1 < steps:
+                for j in range(3):
+                    flip_turn(s + 1, j)
+            exp_shifted(s)
+            sums(s, 1)
+            for j in range(2, 4 if fresh else 2):
+                for f in fresh:
+                    square(f, side, banks[j], 4 * j, 4)
+
+        logarithm(1, 0, K - 1)
+        logarithm(1, K - 1, K)
+        finish(1)

@@ -22,9 +22,9 @@ NQ = Q // P
 GROUPS = (2, 2, 4, 4, 4)
 UNITS = ((0, 2), (2, 1), (3, 2), (5, 2), (7, 2), (9, 2), (11, 2), (13, 2), (15, 2))
 UNITS_OF_GROUP = ((0, 1), (2,), (3, 4), (5, 6), (7, 8))
-RELU_ON_VECTOR = [[],[],[1],[1,3],[1,2,3]]
+RELU_ON_VECTOR = [[],[],[0],[],[0,1,3]]
 COPY_ON_VECTOR = [0,0,0,0,0,0,0,0,0]
-COLLECT_ON_SCALAR = []
+COLLECT_ON_SCALAR = [0,1,2,3,4,5,6,7,8,9,10]
 
 
 def tile_bigramconvkernelpoolingmatch_kernel(tc, q, x_bytes, x_scale, w, bias, gain, mu, sigma, out):
@@ -115,7 +115,7 @@ def tile_bigramconvkernelpoolingmatch_kernel(tc, q, x_bytes, x_scale, w, bias, g
         grouped_w = {}
 
         def w_group(tap):
-            grouped = work.tile([P, T * P, T], BF16, name="w_grouped", align_bytes=64)
+            grouped = work.tile([P, T * P, T], BF16, name="w_grouped", tag="t1", bufs=4, align_bytes=64)
             src = w_raw[tap][:].rearrange("p j (m t) -> p t m j", t=T)
             dst = grouped[:].rearrange("p (t m) j -> p t m j", t=T)
             cut = T if tap == 0 else 2
@@ -193,34 +193,23 @@ def tile_bigramconvkernelpoolingmatch_kernel(tc, q, x_bytes, x_scale, w, bias, g
             nc.vector.quantize_mx(out=d_codes[:, lo : lo + width_n].bitcast(FP8X4), scales=d_scales[:, lo : lo + width_n], in_=grouped_of[g][:, 0:width_n, :].rearrange("p n t -> p (n t)"))
 
         steps = 2 * K
-        us, lows, negs, rs, res, t1s, flips = {}, {}, {}, {}, {}, {}, {}
+        us, lows, rs, t1s = {}, {}, {}, {}
+        res = [keep.tile([P, 2, 2, K, P], F32, name="res%d" % half) for half in range(2)]
 
-        def scores(block, side, first, count):
+        def scores(block, first, count):
             bank = psum.tile([P, 4, P], F32, name="s", tag="s", bufs=3)
             q_cols = slice(block * P, (block + 1) * P)
-            if side == 0:
-                cols = slice(first * B, (first + count) * B)
+            for i in range(count):
+                cols = slice((first + i) * B, (first + i + 1) * B)
                 nc.tensor.matmul_mx(
-                    out=bank[:, 0:count, :],
-                    lhsT=q_codes[:, q_cols].bitcast(FP8X4),
-                    lhsT_scale=q_scales[:, q_cols],
-                    rhs=d_codes[:, cols].bitcast(FP8X4),
-                    rhs_scale=d_scales[:, cols],
+                    out=bank[:, i, :],
+                    lhsT=d_codes[:, cols].bitcast(FP8X4),
+                    lhsT_scale=d_scales[:, cols],
+                    rhs=q_codes[:, q_cols].bitcast(FP8X4),
+                    rhs_scale=q_scales[:, q_cols],
                     start=True,
                     stop=True,
                 )
-            else:
-                for i in range(count):
-                    cols = slice((first + i) * B, (first + i + 1) * B)
-                    nc.tensor.matmul_mx(
-                        out=bank[:, i, :],
-                        lhsT=d_codes[:, cols].bitcast(FP8X4),
-                        lhsT_scale=d_scales[:, cols],
-                        rhs=q_codes[:, q_cols].bitcast(FP8X4),
-                        rhs_scale=q_scales[:, q_cols],
-                        start=True,
-                        stop=True,
-                    )
             return bank
 
         def new_u(s, side):
@@ -232,20 +221,19 @@ def tile_bigramconvkernelpoolingmatch_kernel(tc, q, x_bytes, x_scale, w, bias, g
 
         def first_half(s):
             for side in range(2):
-                t1 = work.tile([P, 2, 4, P], F32, name="t1", bufs=3)
+                t1 = work.tile([P, 2, 4, P], F32, name="t1", tag="t1", bufs=4, align_bytes=64)
                 nc.vector.tensor_tensor(out=t1[:, 0], in0=us[s, side][:, 0:4, :], in1=us[s, side][:, 4:8, :], op=ALU.min)
                 t1s[s, side] = t1
 
-        def level_one(s):
-            for side in range(2):
-                u = us[s, side]
-                if (s, side) in t1s:
-                    nc.vector.tensor_tensor(out=t1s[s, side][:, 1], in0=u[:, 8:12, :], in1=u[:, 12:16, :], op=ALU.min)
-                else:
-                    t1 = work.tile([P, 2, 4, P], F32, name="t1", bufs=3)
-                    v = u[:].rearrange("p (h a n) c -> p h a n c", h=2, a=2)
-                    nc.vector.tensor_tensor(out=t1[:], in0=v[:, :, 0], in1=v[:, :, 1], op=ALU.min)
-                    t1s[s, side] = t1
+        def level_one(s, side):
+            u = us[s, side]
+            if (s, side) in t1s:
+                nc.vector.tensor_tensor(out=t1s[s, side][:, 1], in0=u[:, 8:12, :], in1=u[:, 12:16, :], op=ALU.min)
+            else:
+                t1 = work.tile([P, 2, 4, P], F32, name="t1", tag="t1", bufs=4, align_bytes=64)
+                v = u[:].rearrange("p (h a n) c -> p h a n c", h=2, a=2)
+                nc.vector.tensor_tensor(out=t1[:], in0=v[:, :, 0], in1=v[:, :, 1], op=ALU.min)
+                t1s[s, side] = t1
 
         def levels_two_to_four(s):
             t2s, t3s = [], []
@@ -257,69 +245,50 @@ def tile_bigramconvkernelpoolingmatch_kernel(tc, q, x_bytes, x_scale, w, bias, g
                 t3 = work.tile([P, 2, P], F32, name="t3")
                 nc.vector.tensor_tensor(out=t3[:], in0=t2s[side][:, 0:2, :], in1=t2s[side][:, 2:4, :], op=ALU.min)
                 t3s.append(t3)
-            if s % K == 0:
-                r = keep.tile([P, 4, K, P], F32, name="res%d" % (s // K))
-                res[s // K] = r
-            low0 = res[s // K][:, 3, s % K, :]
-            low1 = work.tile([P, P], F32, name="low", bufs=3)
-            lows[s] = low1
-            neg = work.tile([P, P], F32, name="neg", bufs=3)
-            negs[s] = neg
-            for side, low in ((0, low0), (1, low1[:])):
-                nc.vector.tensor_tensor(out=low, in0=t3s[side][:, 0, :], in1=t3s[side][:, 1, :], op=ALU.min)
-            nc.vector.tensor_scalar(out=neg[:], in0=low0, scalar1=-1.0, scalar2=None, op0=ALU.mult)
+            for side in range(2):
+                low = work.tile([P, P], F32, name="low", bufs=8)
+                nc.vector.tensor_tensor(out=low[:], in0=t3s[side][:, 0, :], in1=t3s[side][:, 1, :], op=ALU.min)
+                lows[s, side] = low
 
-        def shift(s):
-            u = us[s, 1]
-            nc.vector.tensor_tensor(out=u[:], in0=u[:], in1=lows[s][:].unsqueeze(1).to_broadcast([P, N, P]), op=ALU.subtract)
+        def shift(s, side):
+            u = us[s, side]
+            nc.vector.tensor_tensor(out=u[:], in0=u[:], in1=lows[s, side][:].unsqueeze(1).to_broadcast([P, N, P]), op=ALU.subtract)
 
-        def exp_shifted(s):
-            u = us[s, 1]
+        def exponential(s, side):
+            u = us[s, side]
             nc.scalar.activation(out=u[:], in_=u[:], func=ACT.Exp, scale=-1.0)
-
-        def flip_turn(s, j):
-            bank = psum.tile([P, 4, P], F32, name="f", tag="p", bufs=3)
-            for i in range(4):
-                nc.tensor.matmul(out=bank[:, i, :], lhsT=us[s, 0][:, 4 * j + i, :], rhs=ident[:], is_transpose=True, start=True, stop=False)
-                nc.tensor.matmul(out=bank[:, i, :], lhsT=negs[s][:], rhs=ident[:], is_transpose=True, start=False, stop=True)
-            flips[s, j] = bank
-
-        def flip_exp(s, j):
-            nc.scalar.activation(out=us[s, 0][:, 4 * j : 4 * j + 4, :], in_=flips[s, j][:], func=ACT.Exp, scale=-1.0)
 
         def sums(s, side):
             if side == 0:
-                r = psum.tile([P, 3, P], F32, name="r", tag="r", bufs=2)
+                r = psum.tile([P, 2, 2, P], F32, name="r", tag="r", bufs=2)
                 rs[s] = r
-                nc.tensor.transpose(r[:, 2, :], lows[s][:], ident[:])
+            nc.tensor.transpose(rs[s][:, 1, side, :], lows[s, side][:], ident[:])
             for n in range(N):
-                nc.tensor.matmul(out=rs[s][:, side, :], lhsT=us[s, side][:, n, :], rhs=ident[:], is_transpose=True, start=(n == 0), stop=(n == N - 1))
+                nc.tensor.matmul(out=rs[s][:, 0, side, :], lhsT=us[s, side][:, n, :], rhs=ident[:], is_transpose=True, start=(n == 0), stop=(n == N - 1))
 
         def collect(s):
-            o = res[s // K][:, 0:3, s % K, :]
+            half, k = divmod(s, K)
+            o = res[half][:, :, :, k, :]
             if s in COLLECT_ON_SCALAR:
                 nc.scalar.copy(out=o, in_=rs[s][:])
             else:
                 nc.vector.tensor_copy(out=o, in_=rs[s][:])
 
         def logarithm(half, k0, k1):
-            r = res[half]
-            nc.scalar.activation(out=r[:, 0:2, k0:k1, :], in_=r[:, 0:2, k0:k1, :], func=ACT.Ln)
+            r = res[half][:, 0, :, k0:k1, :]
+            nc.scalar.activation(out=r, in_=r, func=ACT.Ln)
 
-        def finish(half):
-            r = res[half]
-            for side, low in ((0, 3), (1, 2)):
-                block = 2 * half + side
-                o = work.tile([P, B, K], F32, name="o")
-                nc.vector.scalar_tensor_tensor(
-                    out=o[:],
-                    in0=r[:, side].rearrange("p k b -> p b k"),
-                    scalar=-math.log(N),
-                    in1=r[:, low].rearrange("p k b -> p b k"),
-                    op0=ALU.add,
-                    op1=ALU.subtract,
-                )
-                nc.sync.dma_start(out=out[block * P : (block + 1) * P], in_=o[:])
+        def finish(block):
+            o = work.tile([P, B, K], F32, name="o")
+            nc.vector.scalar_tensor_tensor(
+                out=o[:],
+                in0=res[block // 2][:, 0, block % 2].rearrange("p k b -> p b k"),
+                scalar=-math.log(N),
+                in1=res[block // 2][:, 1, block % 2].rearrange("p k b -> p b k"),
+                op0=ALU.add,
+                op1=ALU.subtract,
+            )
+            nc.sync.dma_start(out=out[block * P : (block + 1) * P], in_=o[:])
 
         abs_gain = keep.tile([P, T], F32)
         gain_bias = keep.tile([P, T], F32)
@@ -351,7 +320,8 @@ def tile_bigramconvkernelpoolingmatch_kernel(tc, q, x_bytes, x_scale, w, bias, g
         x_quantize(2)
         nc.vector.scalar_tensor_tensor(out=centre[:], in0=mu_bc[:], scalar=-1.0, in1=width[:], op0=ALU.mult, op1=ALU.mult)
         q_late = [q_quantize]
-        for s in range(K):
+        early = 4
+        for s in range(early):
             for side in range(2):
                 new_u(s, side)
 
@@ -370,7 +340,7 @@ def tile_bigramconvkernelpoolingmatch_kernel(tc, q, x_bytes, x_scale, w, bias, g
             d_quantize(g)
             if g == 0:
                 q_quantize()
-            banks = [scores(side, side, first_of[g], GROUPS[g]) for side in range(2)]
+            banks = [scores(side, first_of[g], GROUPS[g]) for side in range(2)]
             if not last:
                 affine_on_vector(g + 1)
             for unit in nxt[1:2]:
@@ -378,61 +348,53 @@ def tile_bigramconvkernelpoolingmatch_kernel(tc, q, x_bytes, x_scale, w, bias, g
                 x_turn(unit)
             for unit in nxt:
                 x_quantize(unit)
-            for s in range(K):
+            for s in range(early):
                 for side in range(2):
                     square(s, side, banks[side], first_of[g], GROUPS[g])
-        for s in range(1):
-            first_half(s)
+            if g + 1 == len(GROUPS):
+                for s in range(2):
+                    first_half(s)
 
+        JOBS = ((0, 0, (4, 5)), (0, 1, (4, 5)), (1, 0, (0, 1)), (1, 1, (0, 1)), (1, 0, (2, 3)), (1, 1, (2, 3)), (1, 0, (4, 5)), (1, 1, (4, 5)))
         def vector_work(s):
             ahead = s + 2
-            if ahead < steps:
-                level_one(ahead)
-            if 0 <= ahead - 1 < steps:
-                shift(ahead - 1)
+            for side in range(2):
+                if ahead < steps:
+                    level_one(ahead, side)
+                if 0 <= ahead - 1 < steps:
+                    shift(ahead - 1, side)
             if ahead < steps:
                 levels_two_to_four(ahead)
-            if 1 <= s <= steps:
-                collect(s - 1)
+            if 2 <= s and s - 2 < steps:
+                collect(s - 2)
 
         for s in range(-2, 0):
             vector_work(s)
-        for j in range(3):
-            flip_turn(0, j)
-        for s in range(steps + 1):
+        for s in range(steps):
             vector_work(s)
-            if s == 8:
+            if s == 9:
                 logarithm(0, 0, K)
-                finish(0)
-            if s == steps:
-                break
+                for block in range(2):
+                    finish(block)
+            job = s - 0
             fresh = []
-            if 1 <= s <= K:
-                base = K + (s - 1) // 2 * 2
-                side = (s - 1) % 2
-                block = 2 + side
-                fresh = [base, base + 1]
+            if 0 <= job < len(JOBS):
+                half, side_new, ks = JOBS[job]
+                fresh = [half * K + k for k in ks]
                 for f in fresh:
-                    new_u(f, side)
-            flip_turn(s, 3)
-            banks = [scores(block, side, 4 * j, 4) for j in range(2)] if fresh else []
-            for j in range(4):
-                flip_exp(s, j)
-            sums(s, 0)
-            for j in range(2 if fresh else 0):
-                for f in fresh:
-                    square(f, side, banks[j], 4 * j, 4)
-            if fresh:
-                banks += [scores(block, side, 4 * j, 4) for j in range(2, 4)]
-            if s + 1 < steps:
-                for j in range(3):
-                    flip_turn(s + 1, j)
-            exp_shifted(s)
-            sums(s, 1)
-            for j in range(2, 4 if fresh else 2):
-                for f in fresh:
-                    square(f, side, banks[j], 4 * j, 4)
+                    new_u(f, side_new)
+            for side in range(2):
+                exponential(s, side)
+                if fresh:
+                    for j in (2 * side, 2 * side + 1):
+                        bank = scores(2 * half + side_new, 4 * j, 4)
+                        for f in fresh:
+                            square(f, side_new, bank, 4 * j, 4)
+                sums(s, side)
+        for s in range(steps, steps + 2):
+            vector_work(s)
 
         logarithm(1, 0, K - 1)
         logarithm(1, K - 1, K)
-        finish(1)
+        for block in range(2, NQ):
+            finish(block)

@@ -17,32 +17,59 @@ ACT = mybir.ActivationFunctionType
 ALU = mybir.AluOpType
 
 P = 128
+
+
+def make_jobs(early):
+    jobs = []
+    s = early
+    if s % 2:
+        jobs.append(((((s,), 0, (0, 1, 2, 3)),), (((s,), 1, (0, 1, 2, 3)),)))
+        s += 1
+    while s < 2 * K:
+        for side in range(2):
+            jobs.append(((((s, s + 1), side, (0, 1)),), (((s, s + 1), side, (2, 3)),)))
+        s += 2
+    return jobs
+
+
 T = 4
 NQ = Q // P
 GROUPS = (2, 2, 4, 4, 4)
 UNITS = ((0, 2), (2, 1), (3, 2), (5, 2), (7, 2), (9, 2), (11, 2), (13, 2), (15, 2))
 UNITS_OF_GROUP = ((0, 1), (2,), (3, 4), (5, 6), (7, 8))
-RELU_ON_VECTOR = [[],[],[0],[],[0,1,3]]
+RELU_ON_VECTOR = [[], [], [], [0, 2], [0, 1, 2]]
 COPY_ON_VECTOR = [0,0,0,0,0,0,0,0,0]
-COLLECT_ON_SCALAR = [0,1,2,3,4,5,6,7,8,9,10]
+COLLECT_ON_SCALAR = [0, 1, 2, 3, 4, 5, 6, 7]
+EARLY = 4
+T1 = 8
+COLLECTED = 8
+WCUT = (4, 3)
+STORE = ("scalar", "vector", "vector", "scalar")
+TURN_LOWS = (8, 10)
+U_BUFS = 12
+SHIFT_PIECES = {(0, 0): 2, (11, 0): 2, (11, 1): 2, (6, 0): 2, (10, 1): 2}
+R_IN_P = (1, 2, 4, 5)
+COLLECTS = {3: (0, 2), 4: (1,), 5: (3,), 7: (4, 5), 9: (6,), 10: (7,)}
+FIRST = ((), (), (), ((0, 0), (0, 1), (1, 0), (1, 1)), ((2, 0), (2, 1), (3, 0), (3, 1)))
 
 
 def tile_bigramconvkernelpoolingmatch_kernel(tc, q, x_bytes, x_scale, w, bias, gain, mu, sigma, out):
     nc = tc.nc
+    jobs = make_jobs(EARLY)
     with ExitStack() as ctx:
         keep = ctx.enter_context(tc.tile_pool(name="keep", bufs=1))
         work = ctx.enter_context(tc.tile_pool(name="work", bufs=2))
-        u_pool = ctx.enter_context(tc.tile_pool(name="u", bufs=12))
+        u_pool = ctx.enter_context(tc.tile_pool(name="u", bufs=U_BUFS))
         psum = ctx.enter_context(tc.psum_pool(name="psum", bufs=3))
         ctx.enter_context(tc.manual_schedule())
 
         x_raw = keep.tile([P, (N + 1) * D], U8)
         x_rows = x_bytes.rearrange("b n d -> b (n d)")
         scale_bc = keep.tile([P, D], F32)
-        w_raw = [keep.tile([P, T, E], BF16, name="w_raw%d" % tap) for tap in range(2)]
+        w_raw = keep.tile([P, 2, T, E], BF16, name="w_raw", tag="w_raw")
         gain_pt = keep.tile([P, T], BF16)
         bias_pt = keep.tile([P, T], BF16)
-        q_rows = keep.tile([P, NQ, E], BF16)
+        q_rows = keep.tile([P, NQ, E], BF16, name="q_rows", tag="q_rows")
         gain_bc = keep.tile([P, E], BF16)
         mu_bc = keep.tile([P, K], BF16)
         sigma_bc = keep.tile([P, K], BF16)
@@ -51,7 +78,7 @@ def tile_bigramconvkernelpoolingmatch_kernel(tc, q, x_bytes, x_scale, w, bias, g
             nc.sync.dma_start(out=x_raw[:, a * D : b * D], in_=x_rows[:, a * D : b * D])
 
         def load_w(tap):
-            nc.sync.dma_start(out=w_raw[tap][:], in_=w[tap].rearrange("(p j) e -> p j e", j=T))
+            nc.sync.dma_start(out=w_raw[:, tap], in_=w[tap].rearrange("(p j) e -> p j e", j=T))
 
         nc.scalar.dma_start(out=scale_bc[:], in_=x_scale.rearrange("a b d -> (a b d)").partition_broadcast(P))
         load_x(0, 3)
@@ -115,11 +142,12 @@ def tile_bigramconvkernelpoolingmatch_kernel(tc, q, x_bytes, x_scale, w, bias, g
         grouped_w = {}
 
         def w_group(tap):
-            grouped = work.tile([P, T * P, T], BF16, name="w_grouped", tag="t1", bufs=4, align_bytes=64)
-            src = w_raw[tap][:].rearrange("p j (m t) -> p t m j", t=T)
+            grouped = work.tile([P, T * P, T], BF16, name="w_grouped", tag="t1", bufs=T1, align_bytes=64)
+            src = w_raw[:, tap].rearrange("p j (m t) -> p t m j", t=T)
             dst = grouped[:].rearrange("p (t m) j -> p t m j", t=T)
-            cut = T if tap == 0 else 2
-            nc.vector.tensor_copy(out=dst[:, 0:cut], in_=src[:, 0:cut])
+            cut = WCUT[tap]
+            if cut > 0:
+                nc.vector.tensor_copy(out=dst[:, 0:cut], in_=src[:, 0:cut])
             if cut < T:
                 nc.scalar.copy(out=dst[:, cut:T], in_=src[:, cut:T])
             grouped_w[tap] = grouped
@@ -193,8 +221,13 @@ def tile_bigramconvkernelpoolingmatch_kernel(tc, q, x_bytes, x_scale, w, bias, g
             nc.vector.quantize_mx(out=d_codes[:, lo : lo + width_n].bitcast(FP8X4), scales=d_scales[:, lo : lo + width_n], in_=grouped_of[g][:, 0:width_n, :].rearrange("p n t -> p (n t)"))
 
         steps = 2 * K
-        us, lows, rs, t1s = {}, {}, {}, {}
-        res = [keep.tile([P, 2, 2, K, P], F32, name="res%d" % half) for half in range(2)]
+        us, rs, t1s = {}, {}, {}
+        res, pairs = [], []
+        lows = keep.tile([P, NQ, K, P], F32, name="lows")
+        lows_turned = {}
+
+        def low_of(s, side):
+            return lows[:, 2 * (s // K) + side, s % K, :]
 
         def scores(block, first, count):
             bank = psum.tile([P, 4, P], F32, name="s", tag="s", bufs=3)
@@ -212,25 +245,24 @@ def tile_bigramconvkernelpoolingmatch_kernel(tc, q, x_bytes, x_scale, w, bias, g
                 )
             return bank
 
-        def new_u(s, side):
-            us[s, side] = u_pool.tile([P, N, P], F32, name="u", tag="u", bufs=12)
-
         def square(s, side, bank, first, count):
             k = s % K
             nc.scalar.activation(out=us[s, side][:, first : first + count, :], in_=bank[:, 0:count, :], func=ACT.Square, bias=centre[:, k : k + 1], scale=width[:, k : k + 1])
 
-        def first_half(s):
-            for side in range(2):
-                t1 = work.tile([P, 2, 4, P], F32, name="t1", tag="t1", bufs=4, align_bytes=64)
-                nc.vector.tensor_tensor(out=t1[:, 0], in0=us[s, side][:, 0:4, :], in1=us[s, side][:, 4:8, :], op=ALU.min)
-                t1s[s, side] = t1
+        def new_u(s, side):
+            us[s, side] = u_pool.tile([P, N, P], F32, name="u", tag="u", bufs=U_BUFS)
+
+        def first_half(s, side):
+            t1 = work.tile([P, 2, 4, P], F32, name="t1", tag="t1", bufs=T1, align_bytes=64)
+            nc.vector.tensor_tensor(out=t1[:, 0], in0=us[s, side][:, 0:4, :], in1=us[s, side][:, 4:8, :], op=ALU.min)
+            t1s[s, side] = t1
 
         def level_one(s, side):
             u = us[s, side]
             if (s, side) in t1s:
                 nc.vector.tensor_tensor(out=t1s[s, side][:, 1], in0=u[:, 8:12, :], in1=u[:, 12:16, :], op=ALU.min)
             else:
-                t1 = work.tile([P, 2, 4, P], F32, name="t1", tag="t1", bufs=4, align_bytes=64)
+                t1 = work.tile([P, 2, 4, P], F32, name="t1", tag="t1", bufs=T1, align_bytes=64)
                 v = u[:].rearrange("p (h a n) c -> p h a n c", h=2, a=2)
                 nc.vector.tensor_tensor(out=t1[:], in0=v[:, :, 0], in1=v[:, :, 1], op=ALU.min)
                 t1s[s, side] = t1
@@ -246,48 +278,74 @@ def tile_bigramconvkernelpoolingmatch_kernel(tc, q, x_bytes, x_scale, w, bias, g
                 nc.vector.tensor_tensor(out=t3[:], in0=t2s[side][:, 0:2, :], in1=t2s[side][:, 2:4, :], op=ALU.min)
                 t3s.append(t3)
             for side in range(2):
-                low = work.tile([P, P], F32, name="low", bufs=8)
-                nc.vector.tensor_tensor(out=low[:], in0=t3s[side][:, 0, :], in1=t3s[side][:, 1, :], op=ALU.min)
-                lows[s, side] = low
+                nc.vector.tensor_tensor(out=low_of(s, side), in0=t3s[side][:, 0, :], in1=t3s[side][:, 1, :], op=ALU.min)
+
+        def pieces(s, side):
+            return SHIFT_PIECES.get((s, side), 1)
 
         def shift(s, side):
             u = us[s, side]
-            nc.vector.tensor_tensor(out=u[:], in0=u[:], in1=lows[s, side][:].unsqueeze(1).to_broadcast([P, N, P]), op=ALU.subtract)
+            step = N // pieces(s, side)
+            for a in range(0, N, step):
+                nc.vector.tensor_tensor(out=u[:, a : a + step, :], in0=u[:, a : a + step, :], in1=low_of(s, side).unsqueeze(1).to_broadcast([P, step, P]), op=ALU.subtract)
 
         def exponential(s, side):
             u = us[s, side]
-            nc.scalar.activation(out=u[:], in_=u[:], func=ACT.Exp, scale=-1.0)
+            step = N // pieces(s, side)
+            for a in range(0, N, step):
+                nc.scalar.activation(out=u[:, a : a + step, :], in_=u[:, a : a + step, :], func=ACT.Exp, scale=-1.0)
 
         def sums(s, side):
             if side == 0:
-                r = psum.tile([P, 2, 2, P], F32, name="r", tag="r", bufs=2)
-                rs[s] = r
-            nc.tensor.transpose(rs[s][:, 1, side, :], lows[s, side][:], ident[:])
+                if s < COLLECTED:
+                    tag, bufs = ("p", 3) if s in R_IN_P else ("r", 2)
+                    rs[s] = psum.tile([P, 2, P], F32, name="r", tag=tag, bufs=bufs)
+                elif (s - COLLECTED) % 2 == 0:
+                    pair = psum.tile([P, 2, 2, P], F32, name="r", tag="r", bufs=2)
+                    rs[s], rs[s + 1] = pair[:, 0], pair[:, 1]
+                    pairs.append(pair)
             for n in range(N):
-                nc.tensor.matmul(out=rs[s][:, 0, side, :], lhsT=us[s, side][:, n, :], rhs=ident[:], is_transpose=True, start=(n == 0), stop=(n == N - 1))
+                nc.tensor.matmul(out=rs[s][:, side, :], lhsT=us[s, side][:, n, :], rhs=ident[:], is_transpose=True, start=(n == 0), stop=(n == N - 1))
 
         def collect(s):
-            half, k = divmod(s, K)
-            o = res[half][:, :, :, k, :]
+            o, i = res[s // K][:, :, s % K, :], rs[s][:, 0:2, :]
             if s in COLLECT_ON_SCALAR:
-                nc.scalar.copy(out=o, in_=rs[s][:])
+                nc.scalar.copy(out=o, in_=i)
             else:
-                nc.vector.tensor_copy(out=o, in_=rs[s][:])
+                nc.vector.tensor_copy(out=o, in_=i)
 
-        def logarithm(half, k0, k1):
-            r = res[half][:, 0, :, k0:k1, :]
-            nc.scalar.activation(out=r, in_=r, func=ACT.Ln)
+        def turn_lows(half):
+            tag = ("s", "p")[half]
+            banks = [psum.tile([P, 4, P], F32, name="low", tag=tag, bufs=3) for i in range(3)]
+            for side in range(2):
+                for k in range(K):
+                    where = banks[side][:, k, :] if k < 4 else banks[2][:, 2 * side + k - 4, :]
+                    nc.tensor.transpose(where, lows[:, 2 * half + side, k, :], ident[:])
+            lows_turned[half] = banks
 
-        def finish(block):
-            o = work.tile([P, B, K], F32, name="o")
-            nc.vector.scalar_tensor_tensor(
-                out=o[:],
-                in0=res[block // 2][:, 0, block % 2].rearrange("p k b -> p b k"),
-                scalar=-math.log(N),
-                in1=res[block // 2][:, 1, block % 2].rearrange("p k b -> p b k"),
-                op0=ALU.add,
-                op1=ALU.subtract,
-            )
+        def logarithm(out, in_):
+            nc.scalar.activation(out=out, in_=in_, func=ACT.Ln, scale=1.0 / N)
+
+        def subtract_lows(half, part):
+            if part < 2:
+                r, low = res[half][:, part, 0:4, :], lows_turned[half][part][:]
+            else:
+                r, low = res[half][:, :, 4:K, :], lows_turned[half][2][:].rearrange("p (a k) c -> p a k c", a=2)
+            nc.vector.tensor_tensor(out=r, in0=r, in1=low, op=ALU.subtract)
+
+        def store(block, engine):
+            half, side = divmod(block, 2)
+            if block < 2:
+                o = work.tile([P, B, K], F32, name="o", tag="relu")
+            else:
+                o = work.tile([P, B, K], F32, name="o", tag="d_grouped", align_bytes=64)
+            i = res[half][:, side].rearrange("p k b -> p b k")
+            if engine == "gpsimd":
+                nc.gpsimd.tensor_scalar(out=o[:], in0=i, scalar1=1.0, scalar2=0.0, op0=ALU.mult, op1=ALU.add)
+            elif engine == "scalar":
+                nc.scalar.copy(out=o[:], in_=i)
+            else:
+                nc.vector.tensor_copy(out=o[:], in_=i)
             nc.sync.dma_start(out=out[block * P : (block + 1) * P], in_=o[:])
 
         abs_gain = keep.tile([P, T], F32)
@@ -296,32 +354,36 @@ def tile_bigramconvkernelpoolingmatch_kernel(tc, q, x_bytes, x_scale, w, bias, g
         width = keep.tile([P, K], F32)
         centre = keep.tile([P, K], F32)
 
-        x_widen(0)
-        x_widen(1)
-        x_turn(0)
-        x_turn(1)
+        for unit in UNITS_OF_GROUP[0]:
+            x_widen(unit)
+        for unit in UNITS_OF_GROUP[0]:
+            x_turn(unit)
         w_group(0)
-        x_quantize(0)
-        x_quantize(1)
+        for unit in UNITS_OF_GROUP[0]:
+            x_quantize(unit)
         w_group(1)
         w_quantize(0)
         nc.vector.scalar_tensor_tensor(out=abs_gain[:], in0=gain_pt[:], scalar=-1.0, in1=gain_pt[:], op0=ALU.mult, op1=ALU.max)
         w_quantize(1)
         nc.vector.tensor_tensor(out=gain_bias[:], in0=abs_gain[:], in1=bias_pt[:], op=ALU.mult)
         nc.vector.tensor_scalar(out=sign_bc[:], in0=gain_bc[:], scalar1=0.0, scalar2=2.0, op0=ALU.is_ge, op1=ALU.mult)
-        x_widen(2)
+        first_unit = UNITS_OF_GROUP[1][0]
+        x_widen(first_unit)
         convolve(0)
-        x_turn(2)
+        x_turn(first_unit)
+        for unit in UNITS_OF_GROUP[1][1:]:
+            x_widen(unit)
+            x_turn(unit)
         nc.vector.tensor_scalar(out=sign_bc[:], in0=sign_bc[:], scalar1=-1.0, scalar2=None, op0=ALU.add)
         nc.vector.reciprocal(out=width[:], in_=sigma_bc[:])
         q_sign()
         q_turn()
         nc.vector.tensor_scalar(out=width[:], in0=width[:], scalar1=math.sqrt(0.5), scalar2=None, op0=ALU.mult)
-        x_quantize(2)
+        for unit in UNITS_OF_GROUP[1]:
+            x_quantize(unit)
+        affine_on_vector(0)
         nc.vector.scalar_tensor_tensor(out=centre[:], in0=mu_bc[:], scalar=-1.0, in1=width[:], op0=ALU.mult, op1=ALU.mult)
-        q_late = [q_quantize]
-        early = 4
-        for s in range(early):
+        for s in range(EARLY):
             for side in range(2):
                 new_u(s, side)
 
@@ -340,7 +402,6 @@ def tile_bigramconvkernelpoolingmatch_kernel(tc, q, x_bytes, x_scale, w, bias, g
             d_quantize(g)
             if g == 0:
                 q_quantize()
-            banks = [scores(side, first_of[g], GROUPS[g]) for side in range(2)]
             if not last:
                 affine_on_vector(g + 1)
             for unit in nxt[1:2]:
@@ -348,14 +409,16 @@ def tile_bigramconvkernelpoolingmatch_kernel(tc, q, x_bytes, x_scale, w, bias, g
                 x_turn(unit)
             for unit in nxt:
                 x_quantize(unit)
-            for s in range(early):
+            banks = [scores(side, first_of[g], GROUPS[g]) for side in range(2)]
+            for s in range(EARLY):
                 for side in range(2):
                     square(s, side, banks[side], first_of[g], GROUPS[g])
-            if g + 1 == len(GROUPS):
-                for s in range(2):
-                    first_half(s)
+            for s, side in FIRST[g]:
+                first_half(s, side)
+            if last:
+                for half in range(2):
+                    res.append(keep.tile([P, 2, K, P], F32, name="res%d" % half, tag=("q_rows", "w_raw")[half]))
 
-        JOBS = ((0, 0, (4, 5)), (0, 1, (4, 5)), (1, 0, (0, 1)), (1, 1, (0, 1)), (1, 0, (2, 3)), (1, 1, (2, 3)), (1, 0, (4, 5)), (1, 1, (4, 5)))
         def vector_work(s):
             ahead = s + 2
             for side in range(2):
@@ -365,36 +428,39 @@ def tile_bigramconvkernelpoolingmatch_kernel(tc, q, x_bytes, x_scale, w, bias, g
                     shift(ahead - 1, side)
             if ahead < steps:
                 levels_two_to_four(ahead)
-            if 2 <= s and s - 2 < steps:
-                collect(s - 2)
+            if s in COLLECTS:
+                for c in COLLECTS[s]:
+                    collect(c)
 
         for s in range(-2, 0):
             vector_work(s)
         for s in range(steps):
             vector_work(s)
-            if s == 9:
-                logarithm(0, 0, K)
-                for block in range(2):
-                    finish(block)
-            job = s - 0
-            fresh = []
-            if 0 <= job < len(JOBS):
-                half, side_new, ks = JOBS[job]
-                fresh = [half * K + k for k in ks]
-                for f in fresh:
-                    new_u(f, side_new)
             for side in range(2):
                 exponential(s, side)
-                if fresh:
-                    for j in (2 * side, 2 * side + 1):
-                        bank = scores(2 * half + side_new, 4 * j, 4)
+                for fresh, side_new, js in jobs[s][side] if s < len(jobs) else ():
+                    for f in fresh:
+                        if (f, side_new) not in us:
+                            new_u(f, side_new)
+                    for j in js:
+                        bank = scores(2 * (fresh[0] // K) + side_new, 4 * j, 4)
                         for f in fresh:
                             square(f, side_new, bank, 4 * j, 4)
                 sums(s, side)
-        for s in range(steps, steps + 2):
-            vector_work(s)
+            for half in range(2):
+                if s == TURN_LOWS[half]:
+                    turn_lows(half)
 
-        logarithm(1, 0, K - 1)
-        logarithm(1, K - 1, K)
-        for block in range(2, NQ):
-            finish(block)
+        for side in range(2):
+            logarithm(res[0][:, side], res[0][:, side])
+            subtract_lows(0, side)
+        logarithm(res[1][:, :, 0 : COLLECTED - K, :], res[1][:, :, 0 : COLLECTED - K, :])
+        for i, pair in enumerate(pairs):
+            k = COLLECTED - K + 2 * i
+            logarithm(res[1][:, :, k : k + 2, :].rearrange("p a k b -> p k a b"), pair[:])
+        subtract_lows(0, 2)
+        store(0, STORE[0])
+        for part in range(3):
+            subtract_lows(1, part)
+        for block in (1, 2, 3):
+            store(block, STORE[block])

@@ -37,19 +37,23 @@ NQ = Q // P
 GROUPS = (2, 2, 4, 4, 4)
 UNITS = ((0, 2), (2, 1), (3, 2), (5, 2), (7, 2), (9, 2), (11, 2), (13, 2), (15, 2))
 UNITS_OF_GROUP = ((0, 1), (2,), (3, 4), (5, 6), (7, 8))
-RELU_ON_VECTOR = [[], [], [], [0, 2], [0, 1, 2]]
+RELU_ON_VECTOR = [[], [], [0], [2], [0, 1, 2]]
 COPY_ON_VECTOR = [0,0,0,0,0,0,0,0,0]
-COLLECT_ON_SCALAR = [0, 1, 2, 3, 4, 5, 6, 7]
+COLLECT_ON_SCALAR = [0, 1, 2, 3, 4, 5, 6, 7, 8, 9]
 EARLY = 4
-T1 = 8
+T1 = 4
+XPLAN = ((2,), (3,), (4,), (), ())
+XLAG = 0
+XBUFS = 3
+SQUARES_FIRST = (2, 5, 6, 7)
 COLLECTED = 8
-WCUT = (4, 3)
-STORE = ("scalar", "vector", "vector", "scalar")
+WCUT = (4, 2)
+STORE = ('gpsimd', 'scalar', 'vector', 'scalar')
 TURN_LOWS = (8, 10)
 U_BUFS = 12
-SHIFT_PIECES = {(0, 0): 2, (11, 0): 2, (11, 1): 2, (6, 0): 2, (10, 1): 2}
-R_IN_P = (1, 2, 4, 5)
-COLLECTS = {3: (0, 2), 4: (1,), 5: (3,), 7: (4, 5), 9: (6,), 10: (7,)}
+SHIFT_PIECES = {(0, 0): 2, (11, 0): 2, (11, 1): 2, (6, 0): 2, (10, 1): 2, (9, 0): 2}
+R_IN_P = (0, 2, 3, 5, 6, 7)
+COLLECTS = {3: (0,), 4: (2,), 5: (1,), 6: (3, 4), 7: (5,), 9: (6,), 11: (7,)}
 FIRST = ((), (), (), ((0, 0), (0, 1), (1, 0), (1, 1)), ((2, 0), (2, 1), (3, 0), (3, 1)))
 
 
@@ -65,12 +69,12 @@ def tile_bigramconvkernelpoolingmatch_kernel(tc, q, x_bytes, x_scale, w, bias, g
 
         x_raw = keep.tile([P, (N + 1) * D], U8)
         x_rows = x_bytes.rearrange("b n d -> b (n d)")
+        scale_pt = keep.tile([P, T], F32)
         scale_bc = keep.tile([P, D], F32)
         w_raw = keep.tile([P, 2, T, E], BF16, name="w_raw", tag="w_raw")
         gain_pt = keep.tile([P, T], BF16)
         bias_pt = keep.tile([P, T], BF16)
         q_rows = keep.tile([P, NQ, E], BF16, name="q_rows", tag="q_rows")
-        gain_bc = keep.tile([P, E], BF16)
         mu_bc = keep.tile([P, K], BF16)
         sigma_bc = keep.tile([P, K], BF16)
 
@@ -80,7 +84,7 @@ def tile_bigramconvkernelpoolingmatch_kernel(tc, q, x_bytes, x_scale, w, bias, g
         def load_w(tap):
             nc.sync.dma_start(out=w_raw[:, tap], in_=w[tap].rearrange("(p j) e -> p j e", j=T))
 
-        nc.scalar.dma_start(out=scale_bc[:], in_=x_scale.rearrange("a b d -> (a b d)").partition_broadcast(P))
+        nc.scalar.dma_start(out=scale_pt[:], in_=x_scale.rearrange("a b (p t) -> (a b p) t", t=T))
         load_x(0, 3)
         load_w(0)
         load_w(1)
@@ -89,9 +93,8 @@ def tile_bigramconvkernelpoolingmatch_kernel(tc, q, x_bytes, x_scale, w, bias, g
         load_x(3, 5)
         nc.sync.dma_start(out=q_rows[:], in_=q.rearrange("(c r) e -> r c e", r=P))
         load_x(5, 9)
-        nc.scalar.dma_start(out=gain_bc[:], in_=gain.partition_broadcast(P))
-        nc.scalar.dma_start(out=mu_bc[:], in_=mu.partition_broadcast(P))
-        nc.scalar.dma_start(out=sigma_bc[:], in_=sigma.partition_broadcast(P))
+        nc.sync.dma_start(out=mu_bc[:], in_=mu.partition_broadcast(P))
+        nc.sync.dma_start(out=sigma_bc[:], in_=sigma.partition_broadcast(P))
         load_x(9, 17)
 
         ident = keep.tile([P, P], F32)
@@ -100,6 +103,14 @@ def tile_bigramconvkernelpoolingmatch_kernel(tc, q, x_bytes, x_scale, w, bias, g
         warm = keep.tile([P, 1], F32)
         nc.vector.memset(warm[:], 1.0)
         nc.scalar.activation(out=warm[:], in_=warm[:], func=ACT.Exp)
+
+        def spread(values):
+            bank = psum.tile([P, T, P], F32, name="bank", tag="r", bufs=2)
+            for t in range(T):
+                nc.tensor.transpose(bank[:, t, :], values[:, t : t + 1].to_broadcast([P, P]), ident[:])
+            return bank[:].rearrange("p t n -> p n t")
+
+        nc.scalar.copy(out=scale_bc[:].rearrange("p (n t) -> p n t", t=T), in_=spread(scale_pt))
 
         def turn(src, count, dst, on_vector):
             xt = psum.tile([P, 2, 2, P], F32, name="xt", tag="p", bufs=3)
@@ -121,7 +132,7 @@ def tile_bigramconvkernelpoolingmatch_kernel(tc, q, x_bytes, x_scale, w, bias, g
 
         def x_widen(unit):
             first, count = UNITS[unit]
-            xs = work.tile([P, 2 * D], BF16, name="xs", bufs=3)
+            xs = work.tile([P, 2 * D], BF16, name="xs", bufs=XBUFS)
             for r in range(count):
                 n = first + r
                 nc.vector.tensor_tensor(out=xs[:, r * D : (r + 1) * D], in0=x_raw[:, n * D : (n + 1) * D].bitcast(FP8), in1=scale_bc[:], op=ALU.mult)
@@ -129,7 +140,7 @@ def tile_bigramconvkernelpoolingmatch_kernel(tc, q, x_bytes, x_scale, w, bias, g
 
         def x_turn(unit):
             count = UNITS[unit][1]
-            xg = work.tile([P, 2 * B * T], BF16, name="xg", bufs=3, align_bytes=64)
+            xg = work.tile([P, 2 * B * T], BF16, name="xg", bufs=XBUFS, align_bytes=64)
             turn(xs_of[unit][:], count, xg[:, 0 : count * B * T], COPY_ON_VECTOR[unit])
             xg_of[unit] = xg
 
@@ -221,7 +232,8 @@ def tile_bigramconvkernelpoolingmatch_kernel(tc, q, x_bytes, x_scale, w, bias, g
             nc.vector.quantize_mx(out=d_codes[:, lo : lo + width_n].bitcast(FP8X4), scales=d_scales[:, lo : lo + width_n], in_=grouped_of[g][:, 0:width_n, :].rearrange("p n t -> p (n t)"))
 
         steps = 2 * K
-        us, rs, t1s = {}, {}, {}
+        us, rs, t1s, t2s, t3s = {}, {}, {}, {}, {}
+        halved = set()
         res, pairs = [], []
         lows = keep.tile([P, NQ, K, P], F32, name="lows")
         lows_turned = {}
@@ -252,42 +264,47 @@ def tile_bigramconvkernelpoolingmatch_kernel(tc, q, x_bytes, x_scale, w, bias, g
         def new_u(s, side):
             us[s, side] = u_pool.tile([P, N, P], F32, name="u", tag="u", bufs=U_BUFS)
 
+        def t1_of(s):
+            if s not in t1s:
+                t1s[s] = work.tile([P, 2, 2, 4, P], F32, name="t1", tag="t1", bufs=T1, align_bytes=64)
+            return t1s[s]
+
         def first_half(s, side):
-            t1 = work.tile([P, 2, 4, P], F32, name="t1", tag="t1", bufs=T1, align_bytes=64)
-            nc.vector.tensor_tensor(out=t1[:, 0], in0=us[s, side][:, 0:4, :], in1=us[s, side][:, 4:8, :], op=ALU.min)
-            t1s[s, side] = t1
+            u = us[s, side]
+            halved.add((s, side))
+            nc.vector.tensor_tensor(out=t1_of(s)[:, side, 0], in0=u[:, 0:4, :], in1=u[:, 4:8, :], op=ALU.min)
 
         def level_one(s, side):
             u = us[s, side]
-            if (s, side) in t1s:
-                nc.vector.tensor_tensor(out=t1s[s, side][:, 1], in0=u[:, 8:12, :], in1=u[:, 12:16, :], op=ALU.min)
+            if (s, side) in halved:
+                nc.vector.tensor_tensor(out=t1_of(s)[:, side, 1], in0=u[:, 8:12, :], in1=u[:, 12:16, :], op=ALU.min)
             else:
-                t1 = work.tile([P, 2, 4, P], F32, name="t1", tag="t1", bufs=T1, align_bytes=64)
                 v = u[:].rearrange("p (h a n) c -> p h a n c", h=2, a=2)
-                nc.vector.tensor_tensor(out=t1[:], in0=v[:, :, 0], in1=v[:, :, 1], op=ALU.min)
-                t1s[s, side] = t1
+                nc.vector.tensor_tensor(out=t1_of(s)[:, side], in0=v[:, :, 0], in1=v[:, :, 1], op=ALU.min)
 
-        def levels_two_to_four(s):
-            t2s, t3s = [], []
-            for side in range(2):
-                t2 = work.tile([P, 4, P], F32, name="t2")
-                nc.vector.tensor_tensor(out=t2[:], in0=t1s[s, side][:, 0], in1=t1s[s, side][:, 1], op=ALU.min)
-                t2s.append(t2)
-            for side in range(2):
-                t3 = work.tile([P, 2, P], F32, name="t3")
-                nc.vector.tensor_tensor(out=t3[:], in0=t2s[side][:, 0:2, :], in1=t2s[side][:, 2:4, :], op=ALU.min)
-                t3s.append(t3)
-            for side in range(2):
-                nc.vector.tensor_tensor(out=low_of(s, side), in0=t3s[side][:, 0, :], in1=t3s[side][:, 1, :], op=ALU.min)
+        def level_two(s, a=0, b=2):
+            if s not in t2s:
+                t2s[s] = work.tile([P, 2, 4, P], F32, name="t2", bufs=1)
+                t3s[s] = work.tile([P, 2, 2, P], F32, name="t3")
+            nc.vector.tensor_tensor(out=t2s[s][:, a:b], in0=t1s[s][:, a:b, 0], in1=t1s[s][:, a:b, 1], op=ALU.min)
+
+        def level_three(s, a=0, b=2):
+            nc.vector.tensor_tensor(out=t3s[s][:, a:b], in0=t2s[s][:, a:b, 0:2, :], in1=t2s[s][:, a:b, 2:4, :], op=ALU.min)
+
+        def level_four(s, a=0, b=2):
+            half, k = divmod(s, K)
+            nc.vector.tensor_tensor(out=lows[:, 2 * half + a : 2 * half + b, k, :], in0=t3s[s][:, a:b, 0, :], in1=t3s[s][:, a:b, 1, :], op=ALU.min)
 
         def pieces(s, side):
             return SHIFT_PIECES.get((s, side), 1)
 
-        def shift(s, side):
+        def shift(s, side, only=None):
             u = us[s, side]
             step = N // pieces(s, side)
-            for a in range(0, N, step):
-                nc.vector.tensor_tensor(out=u[:, a : a + step, :], in0=u[:, a : a + step, :], in1=low_of(s, side).unsqueeze(1).to_broadcast([P, step, P]), op=ALU.subtract)
+            for i in range(pieces(s, side)):
+                if only is None or i == only:
+                    v = u[:, i * step : (i + 1) * step, :]
+                    nc.vector.tensor_tensor(out=v, in0=v, in1=low_of(s, side).unsqueeze(1).to_broadcast([P, step, P]), op=ALU.subtract)
 
         def exponential(s, side):
             u = us[s, side]
@@ -350,6 +367,7 @@ def tile_bigramconvkernelpoolingmatch_kernel(tc, q, x_bytes, x_scale, w, bias, g
 
         abs_gain = keep.tile([P, T], F32)
         gain_bias = keep.tile([P, T], F32)
+        sign_pt = keep.tile([P, T], F32)
         sign_bc = keep.tile([P, E], BF16)
         width = keep.tile([P, K], F32)
         centre = keep.tile([P, K], F32)
@@ -361,12 +379,15 @@ def tile_bigramconvkernelpoolingmatch_kernel(tc, q, x_bytes, x_scale, w, bias, g
         w_group(0)
         for unit in UNITS_OF_GROUP[0]:
             x_quantize(unit)
+        nc.vector.tensor_scalar(out=sign_pt[:], in0=gain_pt[:], scalar1=0.0, scalar2=2.0, op0=ALU.is_ge, op1=ALU.mult)
         w_group(1)
+        nc.vector.tensor_scalar(out=sign_pt[:], in0=sign_pt[:], scalar1=-1.0, scalar2=None, op0=ALU.add)
         w_quantize(0)
+        sign_spread = spread(sign_pt)
         nc.vector.scalar_tensor_tensor(out=abs_gain[:], in0=gain_pt[:], scalar=-1.0, in1=gain_pt[:], op0=ALU.mult, op1=ALU.max)
         w_quantize(1)
         nc.vector.tensor_tensor(out=gain_bias[:], in0=abs_gain[:], in1=bias_pt[:], op=ALU.mult)
-        nc.vector.tensor_scalar(out=sign_bc[:], in0=gain_bc[:], scalar1=0.0, scalar2=2.0, op0=ALU.is_ge, op1=ALU.mult)
+        nc.vector.tensor_copy(out=sign_bc[:].rearrange("p (n t) -> p n t", t=T), in_=sign_spread)
         first_unit = UNITS_OF_GROUP[1][0]
         x_widen(first_unit)
         convolve(0)
@@ -374,7 +395,6 @@ def tile_bigramconvkernelpoolingmatch_kernel(tc, q, x_bytes, x_scale, w, bias, g
         for unit in UNITS_OF_GROUP[1][1:]:
             x_widen(unit)
             x_turn(unit)
-        nc.vector.tensor_scalar(out=sign_bc[:], in0=sign_bc[:], scalar1=-1.0, scalar2=None, op0=ALU.add)
         nc.vector.reciprocal(out=width[:], in_=sigma_bc[:])
         q_sign()
         q_turn()
@@ -387,6 +407,15 @@ def tile_bigramconvkernelpoolingmatch_kernel(tc, q, x_bytes, x_scale, w, bias, g
             for side in range(2):
                 new_u(s, side)
 
+        pending = []
+
+        def feed(unit):
+            x_widen(unit)
+            x_turn(unit)
+            pending.append(unit)
+            if len(pending) > 1:
+                x_quantize(pending.pop(0))
+
         def units_of(g):
             return UNITS_OF_GROUP[g] if g < len(GROUPS) else ()
 
@@ -394,21 +423,19 @@ def tile_bigramconvkernelpoolingmatch_kernel(tc, q, x_bytes, x_scale, w, bias, g
             last = g + 1 == len(GROUPS)
             if not last:
                 convolve(g + 1)
-            nxt = units_of(g + 2)
+            nxt = [u for a in XPLAN[g] for u in units_of(a)]
             d_group(g)
             for unit in nxt[0:1]:
-                x_widen(unit)
-                x_turn(unit)
+                feed(unit)
             d_quantize(g)
             if g == 0:
                 q_quantize()
             if not last:
                 affine_on_vector(g + 1)
-            for unit in nxt[1:2]:
-                x_widen(unit)
-                x_turn(unit)
-            for unit in nxt:
-                x_quantize(unit)
+            for unit in nxt[1:]:
+                feed(unit)
+            while len(pending) > (1 if g + 2 < len(GROUPS) and XLAG else 0):
+                x_quantize(pending.pop(0))
             banks = [scores(side, first_of[g], GROUPS[g]) for side in range(2)]
             for s in range(EARLY):
                 for side in range(2):
@@ -420,32 +447,56 @@ def tile_bigramconvkernelpoolingmatch_kernel(tc, q, x_bytes, x_scale, w, bias, g
                     res.append(keep.tile([P, 2, K, P], F32, name="res%d" % half, tag=("q_rows", "w_raw")[half]))
 
         def vector_work(s):
-            ahead = s + 2
-            for side in range(2):
-                if ahead < steps:
-                    level_one(ahead, side)
-                if 0 <= ahead - 1 < steps:
-                    shift(ahead - 1, side)
-            if ahead < steps:
-                levels_two_to_four(ahead)
-            if s in COLLECTS:
-                for c in COLLECTS[s]:
-                    collect(c)
+            new, old = s + 2, s + 1
+            if new < steps:
+                level_one(new, 0)
+            if 1 <= old < steps:
+                level_four(old)
+            if new < steps:
+                level_one(new, 1)
+            if old < steps:
+                shift(old, 0)
+            if new < steps:
+                level_two(new)
+            if old < steps:
+                shift(old, 1, 0 if new < steps else None)
+            if new < steps:
+                level_three(new)
+                for i in range(1, pieces(old, 1)):
+                    shift(old, 1, i)
+            for c in COLLECTS.get(s, ()):
+                collect(c)
 
-        for s in range(-2, 0):
-            vector_work(s)
+        for side in range(2):
+            level_one(0, side)
+        for level in (level_two, level_three, level_four):
+            for side in range(2):
+                level(0, side, side + 1)
+        vector_work(-1)
+        half_steps = [jobs[h // 2][h % 2] if h // 2 < len(jobs) else () for h in range(2 * steps + 1)]
+
+        def score_banks(h):
+            found = []
+            for fresh, side, js in half_steps[h]:
+                for f in fresh:
+                    if (f, side) not in us:
+                        new_u(f, side)
+                for j in js:
+                    found.append((fresh, side, j, scores(2 * (fresh[0] // K) + side, 4 * j, 4)))
+            return found
+
+        found = score_banks(0)
         for s in range(steps):
             vector_work(s)
             for side in range(2):
-                exponential(s, side)
-                for fresh, side_new, js in jobs[s][side] if s < len(jobs) else ():
+                if s not in SQUARES_FIRST:
+                    exponential(s, side)
+                for fresh, side_new, j, bank in found:
                     for f in fresh:
-                        if (f, side_new) not in us:
-                            new_u(f, side_new)
-                    for j in js:
-                        bank = scores(2 * (fresh[0] // K) + side_new, 4 * j, 4)
-                        for f in fresh:
-                            square(f, side_new, bank, 4 * j, 4)
+                        square(f, side_new, bank, 4 * j, 4)
+                if s in SQUARES_FIRST:
+                    exponential(s, side)
+                found = score_banks(2 * s + side + 1)
                 sums(s, side)
             for half in range(2):
                 if s == TURN_LOWS[half]:

import math
from contextlib import ExitStack

import concourse.mybir as mybir
from concourse.masks import make_identity

Q, B, N, D, E, K = 512, 128, 16, 512, 512, 6
FLOPS = 2 * 2 * (B * N) * D * E + 2 * Q * (B * N) * E

F32 = mybir.dt.float32
BF16 = mybir.dt.bfloat16
U32 = mybir.dt.uint32
U8 = mybir.dt.uint8
FP8 = mybir.dt.float8_e4m3fn
FP8X4 = mybir.dt.float8_e4m3fn_x4
ACT = mybir.ActivationFunctionType
ALU = mybir.AluOpType

P = 128


def make_jobs(early):
    jobs = []
    s = early
    if s % 2:
        jobs.append(((((s,), 0, (0, 1, 2, 3)),), (((s,), 1, (0, 1, 2, 3)),)))
        s += 1
    while s < 2 * K:
        for side in range(2):
            jobs.append(((((s, s + 1), side, (0, 1)),), (((s, s + 1), side, (2, 3)),)))
        s += 2
    return jobs


T = 4
NQ = Q // P
GROUPS = (2, 2, 4, 4, 4)
UNITS = ((0, 2), (2, 1), (3, 2), (5, 2), (7, 2), (9, 2), (11, 2), (13, 2), (15, 2))
UNITS_OF_GROUP = ((0, 1), (2,), (3, 4), (5, 6), (7, 8))
RELU_ON_VECTOR = [[], [], [0], [2], [0, 1, 2]]
COPY_ON_VECTOR = [0,0,0,0,0,0,0,0,0]
COLLECT_ON_SCALAR = [0, 1, 2, 3, 4, 5, 6, 7, 8, 9]
EARLY = 4
T1 = 4
XPLAN = ((2,), (3,), (4,), (), ())
XLAG = 0
XBUFS = 3
SQUARES_FIRST = (2, 5, 6, 7)
COLLECTED = 8
WCUT = (4, 2)
STORE = ('gpsimd', 'scalar', 'vector', 'scalar')
TURN_LOWS = (8, 10)
U_BUFS = 12
SHIFT_PIECES = {(0, 0): 2, (11, 0): 2, (11, 1): 2, (6, 0): 2, (10, 1): 2, (9, 0): 2}
R_IN_P = (0, 2, 3, 5, 6, 7)
COLLECTS = {3: (0,), 4: (2,), 5: (1,), 6: (3, 4), 7: (5,), 9: (6,), 11: (7,)}
FIRST = ((), (), (), ((0, 0), (0, 1), (1, 0), (1, 1)), ((2, 0), (2, 1), (3, 0), (3, 1)))


def tile_bigramconvkernelpoolingmatch_kernel(tc, q, x_bytes, x_scale, w, bias, gain, mu, sigma, out):
    nc = tc.nc
    jobs = make_jobs(EARLY)
    with ExitStack() as ctx:
        keep = ctx.enter_context(tc.tile_pool(name="keep", bufs=1))
        work = ctx.enter_context(tc.tile_pool(name="work", bufs=2))
        u_pool = ctx.enter_context(tc.tile_pool(name="u", bufs=U_BUFS))
        psum = ctx.enter_context(tc.psum_pool(name="psum", bufs=3))
        ctx.enter_context(tc.manual_schedule())

        x_raw = keep.tile([P, (N + 1) * D], U8)
        x_rows = x_bytes.rearrange("b n d -> b (n d)")
        scale_pt = keep.tile([P, T], F32)
        scale_bc = keep.tile([P, D], F32)
        w_raw = keep.tile([P, 2, T, E], BF16, name="w_raw", tag="w_raw")
        gain_pt = keep.tile([P, T], BF16)
        bias_pt = keep.tile([P, T], BF16)
        q_rows = keep.tile([P, NQ, E], BF16, name="q_rows", tag="q_rows")
        mu_bc = keep.tile([P, K], BF16)
        sigma_bc = keep.tile([P, K], BF16)

        def load_x(a, b):
            nc.sync.dma_start(out=x_raw[:, a * D : b * D], in_=x_rows[:, a * D : b * D])

        def load_w(tap):
            nc.sync.dma_start(out=w_raw[:, tap], in_=w[tap].rearrange("(p j) e -> p j e", j=T))

        nc.scalar.dma_start(out=scale_pt[:], in_=x_scale.rearrange("a b (p t) -> (a b p) t", t=T))
        load_x(0, 3)
        load_w(0)
        load_w(1)
        nc.scalar.dma_start(out=gain_pt[:], in_=gain.rearrange("(p t) -> p t", t=T))
        nc.scalar.dma_start(out=bias_pt[:], in_=bias.rearrange("(p t) -> p t", t=T))
        load_x(3, 5)
        nc.sync.dma_start(out=q_rows[:], in_=q.rearrange("(c r) e -> r c e", r=P))
        load_x(5, 9)
        nc.sync.dma_start(out=mu_bc[:], in_=mu.partition_broadcast(P))
        nc.sync.dma_start(out=sigma_bc[:], in_=sigma.partition_broadcast(P))
        load_x(9, 17)

        ident = keep.tile([P, P], F32)
        make_identity(nc, ident[:])

        warm = keep.tile([P, 1], F32)
        nc.vector.memset(warm[:], 1.0)
        nc.scalar.activation(out=warm[:], in_=warm[:], func=ACT.Exp)

        def spread(values):
            bank = psum.tile([P, T, P], F32, name="bank", tag="r", bufs=2)
            for t in range(T):
                nc.tensor.transpose(bank[:, t, :], values[:, t : t + 1].to_broadcast([P, P]), ident[:])
            return bank[:].rearrange("p t n -> p n t")

        nc.scalar.copy(out=scale_bc[:].rearrange("p (n t) -> p n t", t=T), in_=spread(scale_pt))

        def turn(src, count, dst, on_vector):
            xt = psum.tile([P, 2, 2, P], F32, name="xt", tag="p", bufs=3)
            words = src.bitcast(F32)
            for r in range(count):
                base = 256 * r
                for u in range(2):
                    nc.tensor.transpose(xt[:, r, u, :], words[:, base + u : base + 256 : 2], ident[:])
            o = dst.bitcast(F32).rearrange("p (b r u) -> p b r u", b=count, u=2)
            i = xt[:, 0:count].rearrange("p b u r -> p b r u")
            if on_vector:
                nc.vector.tensor_copy(out=o, in_=i)
            else:
                nc.scalar.copy(out=o, in_=i)

        x_codes = keep.tile([P, (N + 1) * B], U32, align_bytes=64)
        x_scales = keep.tile([P, (N + 1) * B], U8, align_bytes=64)
        xs_of, xg_of = {}, {}

        def x_widen(unit):
            first, count = UNITS[unit]
            xs = work.tile([P, 2 * D], BF16, name="xs", bufs=XBUFS)
            for r in range(count):
                n = first + r
                nc.vector.tensor_tensor(out=xs[:, r * D : (r + 1) * D], in0=x_raw[:, n * D : (n + 1) * D].bitcast(FP8), in1=scale_bc[:], op=ALU.mult)
            xs_of[unit] = xs

        def x_turn(unit):
            count = UNITS[unit][1]
            xg = work.tile([P, 2 * B * T], BF16, name="xg", bufs=XBUFS, align_bytes=64)
            turn(xs_of[unit][:], count, xg[:, 0 : count * B * T], COPY_ON_VECTOR[unit])
            xg_of[unit] = xg

        def x_quantize(unit):
            first, count = UNITS[unit]
            cols = slice(first * B, (first + count) * B)
            nc.vector.quantize_mx(out=x_codes[:, cols].bitcast(FP8X4), scales=x_scales[:, cols], in_=xg_of[unit][:, 0 : count * B * T])

        w_codes, w_scales = [], []
        grouped_w = {}

        def w_group(tap):
            grouped = work.tile([P, T * P, T], BF16, name="w_grouped", tag="t1", bufs=T1, align_bytes=64)
            src = w_raw[:, tap].rearrange("p j (m t) -> p t m j", t=T)
            dst = grouped[:].rearrange("p (t m) j -> p t m j", t=T)
            cut = WCUT[tap]
            if cut > 0:
                nc.vector.tensor_copy(out=dst[:, 0:cut], in_=src[:, 0:cut])
            if cut < T:
                nc.scalar.copy(out=dst[:, cut:T], in_=src[:, cut:T])
            grouped_w[tap] = grouped

        def w_quantize(tap):
            codes = keep.tile([P, E], U32, name="w_codes%d" % tap, align_bytes=64)
            scales = keep.tile([P, E], U8, name="w_scales%d" % tap, align_bytes=64)
            nc.vector.quantize_mx(out=codes[:].bitcast(FP8X4), scales=scales[:], in_=grouped_w[tap][:].rearrange("p c j -> p (c j)"))
            w_codes.append(codes)
            w_scales.append(scales)

        q_codes = keep.tile([P, Q], U32, align_bytes=64)
        q_scales = keep.tile([P, Q], U8, align_bytes=64)
        q_parts = {}

        def q_sign():
            qs = work.tile([P, NQ, E], BF16, name="qs", tag="relu")
            nc.vector.tensor_tensor(out=qs[:], in0=q_rows[:], in1=sign_bc[:].unsqueeze(1).to_broadcast([P, NQ, E]), op=ALU.mult)
            qg = work.tile([P, Q * T], BF16, name="qg", tag="d_grouped", align_bytes=64)
            q_parts[0] = (qs, qg)

        def q_turn():
            qs, qg = q_parts[0]
            for h in range(2):
                turn(qs[:, 2 * h : 2 * h + 2, :].rearrange("p c e -> p (c e)"), 2, qg[:, h * 1024 : (h + 1) * 1024], False)

        def q_quantize():
            nc.vector.quantize_mx(out=q_codes[:].bitcast(FP8X4), scales=q_scales[:], in_=q_parts[0][1][:])

        d_codes = keep.tile([P, N * B], U32, align_bytes=64)
        d_scales = keep.tile([P, N * B], U8, align_bytes=64)
        relu_of, grouped_of, h_of = {}, {}, {}
        first_of = [sum(GROUPS[:g]) for g in range(len(GROUPS))]

        def convolve(g):
            width_n = GROUPS[g] * B
            lo = first_of[g] * B
            relu = work.tile([P, T, 4 * B], BF16, name="relu", tag="relu")
            relu_of[g] = relu
            for t in range(T):
                h = psum.tile([P, 4 * B], F32, name="h", tag=("p", "r")[t % 2], bufs=(3, 2)[t % 2])
                for tap in range(2):
                    cols = slice(lo + tap * B, lo + tap * B + width_n)
                    nc.tensor.matmul_mx(
                        out=h[:, 0:width_n],
                        lhsT=w_codes[tap][:, t * P : (t + 1) * P].bitcast(FP8X4),
                        lhsT_scale=w_scales[tap][:, t * P : (t + 1) * P],
                        rhs=x_codes[:, cols].bitcast(FP8X4),
                        rhs_scale=x_scales[:, cols],
                        start=(tap == 0),
                        stop=(tap == 1),
                    )
                h_of[g, t] = h
                if t not in RELU_ON_VECTOR[g]:
                    nc.scalar.activation(out=relu[:, t, 0:width_n], in_=h[:, 0:width_n], func=ACT.Identity, bias=gain_bias[:, t : t + 1], scale=abs_gain[:, t : t + 1])

        def affine_on_vector(g):
            width_n = GROUPS[g] * B
            for t in RELU_ON_VECTOR[g]:
                nc.vector.tensor_scalar(out=relu_of[g][:, t, 0:width_n], in0=h_of[g, t][:, 0:width_n], scalar1=abs_gain[:, t : t + 1], scalar2=gain_bias[:, t : t + 1], op0=ALU.mult, op1=ALU.add)

        def d_group(g):
            width_n = GROUPS[g] * B
            grouped = work.tile([P, 4 * B, T], BF16, name="d_grouped", tag="d_grouped", align_bytes=64)
            nc.vector.tensor_scalar(out=grouped[:, 0:width_n, :], in0=relu_of[g][:, :, 0:width_n].rearrange("p t n -> p n t"), scalar1=0.0, scalar2=None, op0=ALU.max)
            grouped_of[g] = grouped

        def d_quantize(g):
            width_n = GROUPS[g] * B
            lo = first_of[g] * B
            nc.vector.quantize_mx(out=d_codes[:, lo : lo + width_n].bitcast(FP8X4), scales=d_scales[:, lo : lo + width_n], in_=grouped_of[g][:, 0:width_n, :].rearrange("p n t -> p (n t)"))

        steps = 2 * K
        us, rs, t1s, t2s, t3s = {}, {}, {}, {}, {}
        halved = set()
        res, pairs = [], []
        lows = keep.tile([P, NQ, K, P], F32, name="lows")
        lows_turned = {}

        def low_of(s, side):
            return lows[:, 2 * (s // K) + side, s % K, :]

        def scores(block, first, count):
            bank = psum.tile([P, 4, P], F32, name="s", tag="s", bufs=3)
            q_cols = slice(block * P, (block + 1) * P)
            for i in range(count):
                cols = slice((first + i) * B, (first + i + 1) * B)
                nc.tensor.matmul_mx(
                    out=bank[:, i, :],
                    lhsT=d_codes[:, cols].bitcast(FP8X4),
                    lhsT_scale=d_scales[:, cols],
                    rhs=q_codes[:, q_cols].bitcast(FP8X4),
                    rhs_scale=q_scales[:, q_cols],
                    start=True,
                    stop=True,
                )
            return bank

        def square(s, side, bank, first, count):
            k = s % K
            nc.scalar.activation(out=us[s, side][:, first : first + count, :], in_=bank[:, 0:count, :], func=ACT.Square, bias=centre[:, k : k + 1], scale=width[:, k : k + 1])

        def new_u(s, side):
            us[s, side] = u_pool.tile([P, N, P], F32, name="u", tag="u", bufs=U_BUFS)

        def t1_of(s):
            if s not in t1s:
                t1s[s] = work.tile([P, 2, 2, 4, P], F32, name="t1", tag="t1", bufs=T1, align_bytes=64)
            return t1s[s]

        def first_half(s, side):
            u = us[s, side]
            halved.add((s, side))
            nc.vector.tensor_tensor(out=t1_of(s)[:, side, 0], in0=u[:, 0:4, :], in1=u[:, 4:8, :], op=ALU.min)

        def level_one(s, side):
            u = us[s, side]
            if (s, side) in halved:
                nc.vector.tensor_tensor(out=t1_of(s)[:, side, 1], in0=u[:, 8:12, :], in1=u[:, 12:16, :], op=ALU.min)
            else:
                v = u[:].rearrange("p (h a n) c -> p h a n c", h=2, a=2)
                nc.vector.tensor_tensor(out=t1_of(s)[:, side], in0=v[:, :, 0], in1=v[:, :, 1], op=ALU.min)

        def level_two(s, a=0, b=2):
            if s not in t2s:
                t2s[s] = work.tile([P, 2, 4, P], F32, name="t2", bufs=1)
                t3s[s] = work.tile([P, 2, 2, P], F32, name="t3")
            nc.vector.tensor_tensor(out=t2s[s][:, a:b], in0=t1s[s][:, a:b, 0], in1=t1s[s][:, a:b, 1], op=ALU.min)

        def level_three(s, a=0, b=2):
            nc.vector.tensor_tensor(out=t3s[s][:, a:b], in0=t2s[s][:, a:b, 0:2, :], in1=t2s[s][:, a:b, 2:4, :], op=ALU.min)

        def level_four(s, a=0, b=2):
            half, k = divmod(s, K)
            nc.vector.tensor_tensor(out=lows[:, 2 * half + a : 2 * half + b, k, :], in0=t3s[s][:, a:b, 0, :], in1=t3s[s][:, a:b, 1, :], op=ALU.min)

        def pieces(s, side):
            return SHIFT_PIECES.get((s, side), 1)

        def shift(s, side, only=None):
            u = us[s, side]
            step = N // pieces(s, side)
            for i in range(pieces(s, side)):
                if only is None or i == only:
                    v = u[:, i * step : (i + 1) * step, :]
                    nc.vector.tensor_tensor(out=v, in0=v, in1=low_of(s, side).unsqueeze(1).to_broadcast([P, step, P]), op=ALU.subtract)

        def exponential(s, side):
            u = us[s, side]
            step = N // pieces(s, side)
            for a in range(0, N, step):
                nc.scalar.activation(out=u[:, a : a + step, :], in_=u[:, a : a + step, :], func=ACT.Exp, scale=-1.0)

        def sums(s, side):
            if side == 0:
                if s < COLLECTED:
                    tag, bufs = ("p", 3) if s in R_IN_P else ("r", 2)
                    rs[s] = psum.tile([P, 2, P], F32, name="r", tag=tag, bufs=bufs)
                elif (s - COLLECTED) % 2 == 0:
                    pair = psum.tile([P, 2, 2, P], F32, name="r", tag="r", bufs=2)
                    rs[s], rs[s + 1] = pair[:, 0], pair[:, 1]
                    pairs.append(pair)
            for n in range(N):
                nc.tensor.matmul(out=rs[s][:, side, :], lhsT=us[s, side][:, n, :], rhs=ident[:], is_transpose=True, start=(n == 0), stop=(n == N - 1))

        def collect(s):
            o, i = res[s // K][:, :, s % K, :], rs[s][:, 0:2, :]
            if s in COLLECT_ON_SCALAR:
                nc.scalar.copy(out=o, in_=i)
            else:
                nc.vector.tensor_copy(out=o, in_=i)

        def turn_lows(half):
            tag = ("s", "p")[half]
            banks = [psum.tile([P, 4, P], F32, name="low", tag=tag, bufs=3) for i in range(3)]
            for side in range(2):
                for k in range(K):
                    where = banks[side][:, k, :] if k < 4 else banks[2][:, 2 * side + k - 4, :]
                    nc.tensor.transpose(where, lows[:, 2 * half + side, k, :], ident[:])
            lows_turned[half] = banks

        def logarithm(out, in_):
            nc.scalar.activation(out=out, in_=in_, func=ACT.Ln, scale=1.0 / N)

        def subtract_lows(half, part):
            if part < 2:
                r, low = res[half][:, part, 0:4, :], lows_turned[half][part][:]
            else:
                r, low = res[half][:, :, 4:K, :], lows_turned[half][2][:].rearrange("p (a k) c -> p a k c", a=2)
            nc.vector.tensor_tensor(out=r, in0=r, in1=low, op=ALU.subtract)

        def store(block, engine):
            half, side = divmod(block, 2)
            if block < 2:
                o = work.tile([P, B, K], F32, name="o", tag="relu")
            else:
                o = work.tile([P, B, K], F32, name="o", tag="d_grouped", align_bytes=64)
            i = res[half][:, side].rearrange("p k b -> p b k")
            if engine == "gpsimd":
                nc.gpsimd.tensor_scalar(out=o[:], in0=i, scalar1=1.0, scalar2=0.0, op0=ALU.mult, op1=ALU.add)
            elif engine == "scalar":
                nc.scalar.copy(out=o[:], in_=i)
            else:
                nc.vector.tensor_copy(out=o[:], in_=i)
            nc.sync.dma_start(out=out[block * P : (block + 1) * P], in_=o[:])

        abs_gain = keep.tile([P, T], F32)
        gain_bias = keep.tile([P, T], F32)
        sign_pt = keep.tile([P, T], F32)
        sign_bc = keep.tile([P, E], BF16)
        width = keep.tile([P, K], F32)
        centre = keep.tile([P, K], F32)

        for unit in UNITS_OF_GROUP[0]:
            x_widen(unit)
        for unit in UNITS_OF_GROUP[0]:
            x_turn(unit)
        w_group(0)
        for unit in UNITS_OF_GROUP[0]:
            x_quantize(unit)
        nc.vector.tensor_scalar(out=sign_pt[:], in0=gain_pt[:], scalar1=0.0, scalar2=2.0, op0=ALU.is_ge, op1=ALU.mult)
        w_group(1)
        nc.vector.tensor_scalar(out=sign_pt[:], in0=sign_pt[:], scalar1=-1.0, scalar2=None, op0=ALU.add)
        w_quantize(0)
        sign_spread = spread(sign_pt)
        nc.vector.scalar_tensor_tensor(out=abs_gain[:], in0=gain_pt[:], scalar=-1.0, in1=gain_pt[:], op0=ALU.mult, op1=ALU.max)
        w_quantize(1)
        nc.vector.tensor_tensor(out=gain_bias[:], in0=abs_gain[:], in1=bias_pt[:], op=ALU.mult)
        nc.vector.tensor_copy(out=sign_bc[:].rearrange("p (n t) -> p n t", t=T), in_=sign_spread)
        first_unit = UNITS_OF_GROUP[1][0]
        x_widen(first_unit)
        convolve(0)
        x_turn(first_unit)
        for unit in UNITS_OF_GROUP[1][1:]:
            x_widen(unit)
            x_turn(unit)
        nc.vector.reciprocal(out=width[:], in_=sigma_bc[:])
        q_sign()
        q_turn()
        nc.vector.tensor_scalar(out=width[:], in0=width[:], scalar1=math.sqrt(0.5), scalar2=None, op0=ALU.mult)
        for unit in UNITS_OF_GROUP[1]:
            x_quantize(unit)
        affine_on_vector(0)
        nc.vector.scalar_tensor_tensor(out=centre[:], in0=mu_bc[:], scalar=-1.0, in1=width[:], op0=ALU.mult, op1=ALU.mult)
        for s in range(EARLY):
            for side in range(2):
                new_u(s, side)

        pending = []

        def feed(unit):
            x_widen(unit)
            x_turn(unit)
            pending.append(unit)
            if len(pending) > 1:
                x_quantize(pending.pop(0))

        def units_of(g):
            return UNITS_OF_GROUP[g] if g < len(GROUPS) else ()

        for g in range(len(GROUPS)):
            last = g + 1 == len(GROUPS)
            if not last:
                convolve(g + 1)
            nxt = [u for a in XPLAN[g] for u in units_of(a)]
            d_group(g)
            for unit in nxt[0:1]:
                feed(unit)
            d_quantize(g)
            if g == 0:
                q_quantize()
            if not last:
                affine_on_vector(g + 1)
            for unit in nxt[1:]:
                feed(unit)
            while len(pending) > (1 if g + 2 < len(GROUPS) and XLAG else 0):
                x_quantize(pending.pop(0))
            banks = [scores(side, first_of[g], GROUPS[g]) for side in range(2)]
            for s in range(EARLY):
                for side in range(2):
                    square(s, side, banks[side], first_of[g], GROUPS[g])
            for s, side in FIRST[g]:
                first_half(s, side)
            if last:
                for half in range(2):
                    res.append(keep.tile([P, 2, K, P], F32, name="res%d" % half, tag=("q_rows", "w_raw")[half]))

        def vector_work(s):
            new, old = s + 2, s + 1
            if new < steps:
                level_one(new, 0)
            if 1 <= old < steps:
                level_four(old)
            if new < steps:
                level_one(new, 1)
            if old < steps:
                shift(old, 0)
            if new < steps:
                level_two(new)
            if old < steps:
                shift(old, 1, 0 if new < steps else None)
            if new < steps:
                level_three(new)
                for i in range(1, pieces(old, 1)):
                    shift(old, 1, i)
            for c in COLLECTS.get(s, ()):
                collect(c)

        for side in range(2):
            level_one(0, side)
        for level in (level_two, level_three, level_four):
            for side in range(2):
                level(0, side, side + 1)
        vector_work(-1)
        half_steps = [jobs[h // 2][h % 2] if h // 2 < len(jobs) else () for h in range(2 * steps + 1)]

        def score_banks(h):
            found = []
            for fresh, side, js in half_steps[h]:
                for f in fresh:
                    if (f, side) not in us:
                        new_u(f, side)
                for j in js:
                    found.append((fresh, side, j, scores(2 * (fresh[0] // K) + side, 4 * j, 4)))
            return found

        found = score_banks(0)
        for s in range(steps):
            vector_work(s)
            for side in range(2):
                if s not in SQUARES_FIRST:
                    exponential(s, side)
                for fresh, side_new, j, bank in found:
                    for f in fresh:
                        square(f, side_new, bank, 4 * j, 4)
                if s in SQUARES_FIRST:
                    exponential(s, side)
                found = score_banks(2 * s + side + 1)
                sums(s, side)
            for half in range(2):
                if s == TURN_LOWS[half]:
                    turn_lows(half)

        for side in range(2):
            logarithm(res[0][:, side], res[0][:, side])
            subtract_lows(0, side)
        logarithm(res[1][:, :, 0 : COLLECTED - K, :], res[1][:, :, 0 : COLLECTED - K, :])
        for i, pair in enumerate(pairs):
            k = COLLECTED - K + 2 * i
            logarithm(res[1][:, :, k : k + 2, :].rearrange("p a k b -> p k a b"), pair[:])
        subtract_lows(0, 2)
        store(0, STORE[0])
        for part in range(3):
            subtract_lows(1, part)
        for block in (1, 2, 3):
            store(block, STORE[block])
